import numpy as np
import ml_dtypes


def mxq(x, axis, fmt="e4m3"):
    dtype, down = {"e4m3": (ml_dtypes.float8_e4m3fn, 7), "e5m2": (ml_dtypes.float8_e5m2, 14)}[fmt]
    v = np.moveaxis(np.asarray(x, np.float32).astype(ml_dtypes.bfloat16).astype(np.float64), axis, -1)
    blocks = v.reshape(v.shape[:-1] + (-1, 32))
    amax = np.abs(blocks).max(-1, keepdims=True)
    byte = np.maximum(np.where(amax > 0, np.frexp(amax)[1] - 1 + 127, 0) - down, 1)
    scale = np.exp2(byte - 127.0)
    codes = (blocks / scale).astype(np.float32).astype(dtype).astype(np.float64)
    return np.moveaxis((codes * scale).reshape(v.shape), -1, axis)


WIDE = False


def mx_kscale(k):
    if not WIDE:
        return np.ones(k)
    levels = np.array([10, -10, 5, -5, 0])
    if k % 512:
        return np.exp2(np.random.permutation(np.resize(levels, k // 32))).repeat(32)
    a = np.empty((k // 512, 16))
    for p in range(k // 512):
        a[p, :8] = np.random.permutation(np.resize(levels, 8))
        for g in range(8):
            far = levels[np.abs(levels - a[p, g]) >= 10]
            a[p, g + 8] = far[np.random.randint(len(far))]
    return np.exp2(a.ravel()).repeat(32)


BF16 = ml_dtypes.bfloat16


def bf(x):
    return np.asarray(x, np.float32).astype(BF16)


def f64(x):
    return np.asarray(x).astype(np.float64)


E2M1 = np.array([0.0, 0.5, 1.0, 1.5, 2.0, 3.0, 4.0, 6.0, -0.0, -0.5, -1.0, -1.5, -2.0, -3.0, -4.0, -6.0])


def pack_weight(w, fmt):
    k, n = w.shape
    w = f64(bf(w)).reshape(k // 32, 32, n)
    amax = np.abs(w).max(1)
    if fmt == "e4m3":
        byte = np.frexp(amax)[1] - 1 + 127 - 7
    else:
        mant, ex = np.frexp(amax / 6.0)
        byte = np.where(mant > 0.5, ex, ex - 1) + 127
    byte = np.clip(np.where(amax > 0, byte, 1), 1, 254)
    scaled = (w * np.exp2(127.0 - byte)[:, None, :]).reshape(k, n).astype(np.float32)
    by_word = np.ascontiguousarray(scaled.reshape(k // 512, 128, 4, n).transpose(0, 1, 3, 2))
    if fmt == "e4m3":
        words = by_word.astype(ml_dtypes.float8_e4m3fn).view(np.uint8)
    else:
        c = by_word.astype(ml_dtypes.float4_e2m1fn).view(np.uint8) & 0xF
        words = c[..., 0::2] | (c[..., 1::2] << 4)
    return np.ascontiguousarray(words), np.ascontiguousarray(byte.astype(np.uint8).reshape(k // 512, 16, n))


def unpack_weight(words, scales, fmt):
    g, p, n, _ = words.shape
    if fmt == "e4m3":
        vals = np.ascontiguousarray(words).view(ml_dtypes.float8_e4m3fn).astype(np.float64)
    else:
        nib = np.empty((g, p, n, 4), np.uint8)
        nib[..., 0::2] = words & 0xF
        nib[..., 1::2] = words >> 4
        vals = E2M1[nib]
    vals = vals * np.repeat(np.exp2(scales.astype(np.float64) - 127.0), 8, axis=1)[..., None]
    return vals.transpose(0, 1, 3, 2).reshape(g * 512, n)
def pack4(w):
    words, scales = pack_weight(w, "e2m1")
    return words.reshape(words.shape[0], 128, -1), scales


def unpack4(words, scales):
    return unpack_weight(words.reshape(words.shape[0], 128, -1, 2), scales, "e2m1")


E4M3FN = np.array([(-1.0 if i & 128 else 1.0) * ((1.0 + (i & 7) / 8.0) * 2.0 ** (((i >> 3) & 15) - 7) if i & 120 else (i & 7) * 2.0 ** -9) for i in range(256)])


def e4m3fn_bytes(y):
    return np.clip(np.asarray(y, np.float64), -448.0, 448.0).astype(np.float32).astype(ml_dtypes.float8_e4m3fn).view(np.uint8)


def e4m3fn_values(b):
    return E4M3FN[b]


F, J, D, A, H, T = 1024, 1024, 1024, 512, 4, 512


def scale_heads(q, head_w):
    n_feat, n_cols = q.shape
    n_heads = head_w.shape[0]
    per_head = q.reshape(n_feat, n_heads, n_cols // n_heads)
    return (per_head * head_w[None, :, None]).reshape(n_feat, n_cols)


def draw0():
    s, u = mx_kscale(D), mx_kscale(D)
    t = mx_kscale(A)
    r = mx_kscale(T)
    dq = bf(np.random.standard_normal((F, D)) * s)
    dk = bf(np.random.standard_normal((J, D)) * u)
    wq_words, wq_scales = pack4(np.random.standard_normal((D, A)) / np.sqrt(D) / s[:, None] * t)
    wk_words, wk_scales = pack4(np.random.standard_normal((D, A)) / np.sqrt(D) / u[:, None] / t)
    return {
        "dq": dq,
        "dk": dk,
        "wq_words": wq_words,
        "wq_scales": wq_scales,
        "wk_words": wk_words,
        "wk_scales": wk_scales,
        "head_w": bf(1.0 + 0.25 * np.random.standard_normal(H)),
        "aq": bf(np.random.standard_normal((T, F)) * T**0.25 * r[:, None]),
        "ak": bf(np.random.standard_normal((T, J)) * T**0.25 / r[:, None]),
        "g": bf(np.random.standard_normal(T)),
    }


def core(dq, dk, wq_words, wq_scales, wk_words, wk_scales, head_w, aq, ak, g):
    n_pairs = aq.shape[0]
    head_dim = wq_scales.shape[2] // head_w.shape[0]

    q = mxq(f64(dq), 1, "e4m3") @ unpack4(wq_words, wq_scales)
    k = mxq(f64(dk), 1, "e4m3") @ unpack4(wk_words, wk_scales)

    qw = scale_heads(q, f64(head_w))

    m = (mxq(qw, 1, "e4m3") @ mxq(k.T, 0, "e4m3")) / np.sqrt(head_dim)

    c = (mxq(f64(aq).T, 1, "e4m3") @ mxq(f64(g)[:, None] * f64(ak), 0, "e4m3")) / n_pairs

    return m * c


def setup_inputs():
    drawn = draw0()
    full = np.asarray(drawn['dq']).astype(np.float64)
    scale = (np.abs(full).reshape(8, 128, 8, 128).max(axis=(1, 3)) / 448.0).astype(np.float32)
    given = {}
    for key, value in drawn.items():
        if key == 'dq':
            given['dq_bytes'] = e4m3fn_bytes(full / np.repeat(np.repeat(scale.astype(np.float64), 128, axis=0), 128, axis=1))
            given['dq_scale'] = scale
        else:
            given[key] = value
    return given


def reference(dq_bytes, dq_scale, dk, wq_words, wq_scales, wk_words, wk_scales, head_w, aq, ak, g):
    return core(e4m3fn_values(dq_bytes) * np.repeat(np.repeat(dq_scale.astype(np.float64), 128, axis=0), 128, axis=1), dk, wq_words, wq_scales, wk_words, wk_scales, head_w, aq, ak, g)

@@ -1,0 +1,311 @@
+import math
+from contextlib import ExitStack
+
+import concourse.mybir as mybir
+from concourse.masks import make_identity
+
+N_FEAT = 1024
+WIDTH = 1024
+CHANNELS = 512
+HEADS = 4
+TOKENS = 512
+FLOPS = 2 * N_FEAT * (2 * WIDTH * CHANNELS + N_FEAT * CHANNELS + N_FEAT * TOKENS)
+
+F32 = mybir.dt.float32
+BF16 = mybir.dt.bfloat16
+I32 = mybir.dt.int32
+U32 = mybir.dt.uint32
+U8 = mybir.dt.uint8
+FP8 = mybir.dt.float8_e4m3fn
+FP8X4 = mybir.dt.float8_e4m3fn_x4
+FP4X4 = mybir.dt.float4_e2m1fn_x4
+MULT = mybir.AluOpType.mult
+COPY = mybir.ActivationFunctionType.Copy
+
+P = 128
+PACK = 4
+HALF = 512
+TILES = N_FEAT // P
+CHAIN = [(side, pair) for pair in range(TILES // 2) for side in ("k", "q")]
+PIECES = [(i, j) for j in range(2) for i in range(TILES)]
+FIRST_PIECE_STEP = 6
+
+
+def tile_featurepairqkscoreattribution_d2p_kernel(
+    tc, dq_bytes, dq_scale, dk, wq_words, wq_scales, wk_words, wk_scales, head_w, aq, ak, g, out
+):
+    nc = tc.nc
+    with ExitStack() as ctx:
+        keep = ctx.enter_context(tc.tile_pool(name="keep", bufs=1))
+        work = ctx.enter_context(tc.tile_pool(name="work", bufs=4))
+        psum = ctx.enter_context(tc.psum_pool(name="psum", bufs=8))
+        ctx.enter_context(tc.manual_schedule())
+
+        ident = keep.tile([P, P], F32, name="ident")
+        dk_in = [keep.tile([P, WIDTH], BF16, name="dk_in%d" % i) for i in range(TILES)]
+        dq_in = [keep.tile([P, 2, WIDTH], U8, name="dq_in%d" % s) for s in range(TILES // 2)]
+        dq_sc = keep.tile([P, 64], F32, name="dq_sc")
+        aq_in = [keep.tile([P, PACK, HALF], BF16, name="aq_in%d" % h) for h in range(2)]
+        ak_in = [keep.tile([P, PACK, HALF], BF16, name="ak_in%d" % h) for h in range(2)]
+        g_in = keep.tile([P, PACK], BF16, name="g_in")
+        head_in = keep.tile([P, HEADS], BF16, name="head_in")
+        head_col = keep.tile([P, 1], F32, name="head_col")
+        words_in, words, scales_in, scales = {}, {}, {}, {}
+        for side in ("k", "q"):
+            words_in[side] = keep.tile([P, 512], I32, name="words_in_" + side, align_bytes=64)
+            words[side] = keep.tile([P, 512], I32, name="words_" + side, align_bytes=64)
+            scales_in[side] = keep.tile([P, 256], I32, name="scales_in_" + side, align_bytes=64)
+            scales[side] = keep.tile([P, 256], I32, name="scales_" + side, align_bytes=64)
+        codes2, scales2 = {}, {}
+        for name in ("k", "q", "aq", "ak"):
+            codes2[name] = keep.tile([P, N_FEAT], U32, name="codes2_" + name, align_bytes=64)
+            scales2[name] = keep.tile([P, N_FEAT], U8, name="scales2_" + name, align_bytes=64)
+
+        for side in ("k", "q"):
+            nc.vector.memset(scales_in[side][:], 0)
+        make_identity(nc, ident[:])
+
+        def load_dk(i):
+            nc.sync.dma_start(out=dk_in[i][:], in_=dk[P * i : P * i + P, :])
+
+        def load_dq(s):
+            rows = dq_bytes[2 * P * s : 2 * P * s + 2 * P, :]
+            nc.sync.dma_start(out=dq_in[s][:], in_=rows.rearrange("(a p) k -> p a k", p=P))
+
+        def load_tokens(dst, src, h):
+            cols = src[:, HALF * h : HALF * h + HALF]
+            nc.sync.dma_start(out=dst[h][:], in_=cols.rearrange("(p t) w -> p t w", t=PACK))
+
+        def load_words(side, src):
+            nc.sync.dma_start(
+                out=words_in[side][:].rearrange("p (g n) -> p g n", g=2),
+                in_=src.bitcast(I32).rearrange("g p n -> p g n"),
+            )
+
+        def load_scales(queue, side, src):
+            rows = src.bitcast(I32)
+            for quad in range(4):
+                queue.dma_start(
+                    out=scales_in[side][32 * quad : 32 * quad + 4, :].rearrange("r (g n) -> r g n", g=2),
+                    in_=rows[:, 4 * quad : 4 * quad + 4, :].rearrange("g r n -> r g n"),
+                )
+
+        load_dk(0)
+        load_dq(0)
+        nc.scalar.dma_start(out=dq_sc[:], in_=dq_scale.rearrange("i j -> (i j)").partition_broadcast(P))
+        load_dk(1)
+        load_scales(nc.scalar, "k", wk_scales)
+        load_words("k", wk_words)
+        load_dk(2)
+        load_dk(3)
+        load_dq(1)
+        load_words("q", wq_words)
+        load_scales(nc.sync, "q", wq_scales)
+        load_tokens(aq_in, aq, 0)
+        load_dk(4)
+        nc.sync.dma_start(out=g_in[:], in_=g.rearrange("(p t) -> p t", t=PACK))
+        nc.sync.dma_start(out=head_in[:], in_=head_w.partition_broadcast(P))
+        load_dk(5)
+        load_dq(2)
+        load_tokens(ak_in, ak, 0)
+        load_dk(6)
+        load_dk(7)
+        load_dq(3)
+        load_tokens(aq_in, aq, 1)
+        load_tokens(ak_in, ak, 1)
+
+        def order_channels(side):
+            for dst, src, run in ((words, words_in, 4), (scales, scales_in, 2)):
+                nc.vector.tensor_copy(
+                    out=dst[side][:].rearrange("p (t x w) -> p t x w", t=4, w=run),
+                    in_=src[side][:].rearrange("p (x t w) -> p t x w", t=4, w=run),
+                )
+
+        def spread_heads():
+            for h in range(HEADS):
+                rows = slice(32 * h, 32 * h + 32)
+                nc.scalar.copy(out=head_col[rows, 0:1], in_=head_in[rows, h : h + 1])
+
+        dq_wide, first_in, first_q, second_in, bank_of = {}, {}, {}, {}, {}
+
+        def widen(i):
+            dq_wide[i] = work.tile([P, WIDTH], BF16, name="wide", bufs=8)
+            by_pass = dq_wide[i][:].rearrange("p (g u m e) -> p g m u e", g=2, u=2, e=2)
+            for j in range(8):
+                nc.vector.tensor_scalar(
+                    out=by_pass[:, j // 4, 32 * (j % 4) : 32 * (j % 4) + 32, :, :],
+                    in0=dq_in[i // 2][:, i % 2, P * j : P * j + P].bitcast(FP8),
+                    scalar1=dq_sc[:, 8 * i + j : 8 * i + j + 1],
+                    scalar2=None,
+                    op0=MULT,
+                )
+
+        def transpose(side, i):
+            pairs = (dk_in[i] if side == "k" else dq_wide[i])[:].bitcast(F32)
+            bank = psum.tile([P, HALF], F32, name="bank")
+            for gg in range(2):
+                for u in range(2):
+                    at = P * (2 * gg + u)
+                    if side == "k":
+                        src = pairs[:, 2 * P * gg + u : 2 * P * gg + 2 * P : 2]
+                    else:
+                        src = pairs[:, at : at + P]
+                    nc.tensor.transpose(bank[:, at : at + P], src, ident[:])
+            bank_of[side, i] = bank
+
+        def collect(side, i):
+            if (side, i // 2) not in first_in:
+                first_in[side, i // 2] = work.tile([P, 2048], BF16, name="first_in", bufs=4, align_bytes=64)
+            dst = first_in[side, i // 2][:, 1024 * (i % 2) : 1024 * (i % 2) + 1024]
+            nc.scalar.copy(
+                out=dst.bitcast(F32).rearrange("p (g f u) -> p g f u", g=2, u=2),
+                in_=bank_of[side, i][:].rearrange("p (g u f) -> p g f u", g=2, u=2),
+            )
+
+        def quantize_first(side, s):
+            codes = work.tile([P, 512], U32, name="codes1", bufs=6, align_bytes=64)
+            sc = work.tile([P, 512], U8, name="scales1", bufs=6, align_bytes=64)
+            nc.vector.quantize_mx(out=codes[:].bitcast(FP8X4), scales=sc[:], in_=first_in[side, s][:])
+            first_q[side, s] = (codes, sc)
+
+        def project(side, i):
+            codes, sc = first_q[side, i // 2]
+            bank = psum.tile([P, HALF], F32, name="bank")
+            for t in range(PACK):
+                for gg in range(2):
+                    at = P * (2 * (i % 2) + gg)
+                    nc.tensor.matmul_mx(
+                        out=bank[:, P * t : P * t + P],
+                        lhsT=words[side][:, 128 * t + 64 * gg : 128 * t + 64 * gg + 64].bitcast(FP4X4),
+                        lhsT_scale=scales[side][:, 64 * t + 32 * gg : 64 * t + 32 * gg + 32].bitcast(U8),
+                        rhs=codes[:, at : at + P].bitcast(FP8X4),
+                        rhs_scale=sc[:, at : at + P],
+                        start=(gg == 0),
+                        stop=(gg == 1),
+                    )
+            bank_of[side, i] = bank
+
+        def round_projection(side, i):
+            if (side, i // 2) not in second_in:
+                second_in[side, i // 2] = work.tile([P, 2, HALF], BF16, name="second_in", bufs=4, align_bytes=64)
+            dst = second_in[side, i // 2][:, i % 2, :].rearrange("p (f t) -> p f t", t=PACK)
+            src = bank_of[side, i][:].rearrange("p (t f) -> p f t", t=PACK)
+            if side == "k":
+                nc.scalar.copy(out=dst, in_=src)
+            else:
+                nc.scalar.activation(out=dst, in_=src, func=COPY, scale=head_col[:, 0:1])
+
+        def quantize_second(side, s):
+            cols = slice(2 * P * s, 2 * P * s + 2 * P)
+            nc.vector.quantize_mx(
+                out=codes2[side][:, cols].bitcast(FP8X4),
+                scales=scales2[side][:, cols],
+                in_=second_in[side, s][:].rearrange("p a c -> p (a c)"),
+            )
+
+        ak_g, side_by_side = {}, {}
+
+        def multiply_g(h):
+            ak_g[h] = work.tile([P, PACK, HALF], BF16, name="ak_g", bufs=2)
+            for t in range(PACK):
+                nc.vector.tensor_scalar(
+                    out=ak_g[h][:, t, :], in0=ak_in[h][:, t, :], scalar1=g_in[:, t : t + 1], scalar2=None, op0=MULT
+                )
+
+        def interleave(name, h, part, copy):
+            if (name, h) not in side_by_side:
+                side_by_side[name, h] = work.tile([P, 2048], BF16, name="side_by_side", bufs=4, align_bytes=64)
+            src = aq_in[h] if name == "aq" else ak_g[h]
+            copy(
+                out=side_by_side[name, h][:, 1024 * part : 1024 * part + 1024].rearrange(
+                    "p (c i t) -> p c t i", i=4, t=PACK
+                ),
+                in_=src[:, :, 256 * part : 256 * part + 256].rearrange("p t (c i) -> p c t i", i=4),
+            )
+
+        def quantize_tokens(name, h):
+            cols = slice(HALF * h, HALF * h + HALF)
+            nc.vector.quantize_mx(
+                out=codes2[name][:, cols].bitcast(FP8X4), scales=scales2[name][:, cols], in_=side_by_side[name, h][:]
+            )
+
+        divisor = 1.0 / (TOKENS * math.sqrt(CHANNELS // HEADS))
+        c_part = {}
+
+        def product(rows, cols, i, j):
+            bank = psum.tile([P, HALF], F32, name="bank")
+            nc.tensor.matmul_mx(
+                out=bank[:],
+                lhsT=codes2[rows][:, P * i : P * i + P].bitcast(FP8X4),
+                lhsT_scale=scales2[rows][:, P * i : P * i + P],
+                rhs=codes2[cols][:, HALF * j : HALF * j + HALF].bitcast(FP8X4),
+                rhs_scale=scales2[cols][:, HALF * j : HALF * j + HALF],
+                start=True,
+                stop=True,
+            )
+            return bank
+
+        def begin_piece(i, j):
+            bank = product("aq", "ak", i, j)
+            c_part[i, j] = work.tile([P, HALF], F32, name="c_part", bufs=8)
+            nc.scalar.activation(out=c_part[i, j][:], in_=bank[:], func=COPY, scale=divisor)
+
+        def finish_piece(i, j):
+            bank = product("q", "k", i, j)
+            piece = work.tile([P, HALF], F32, name="piece", bufs=8)
+            nc.vector.tensor_tensor(out=piece[:], in0=bank[:], in1=c_part[i, j][:], op=MULT)
+            nc.sync.dma_start(out=out[P * i : P * i + P, HALF * j : HALF * j + HALF], in_=piece[:])
+
+        on_vector, on_scalar = nc.vector.tensor_copy, nc.scalar.copy
+        job_in_front = {
+            1: lambda: order_channels("k"),
+            2: lambda: order_channels("q"),
+            3: lambda: interleave("aq", 0, 1, on_vector),
+            4: lambda: multiply_g(0),
+            5: lambda: interleave("ak", 0, 1, on_vector),
+            7: lambda: interleave("aq", 1, 1, on_vector),
+            8: lambda: multiply_g(1),
+            9: lambda: interleave("ak", 1, 1, on_vector),
+        }
+        job_behind = {
+            2: lambda: interleave("aq", 0, 0, on_scalar),
+            3: lambda: quantize_tokens("aq", 0),
+            4: lambda: interleave("ak", 0, 0, on_vector),
+            5: lambda: quantize_tokens("ak", 0),
+            6: lambda: interleave("aq", 1, 0, on_scalar),
+            7: lambda: quantize_tokens("aq", 1),
+            8: lambda: interleave("ak", 1, 0, on_vector),
+            9: lambda: quantize_tokens("ak", 1),
+        }
+
+        for s in range(FIRST_PIECE_STEP + len(PIECES) + 1):
+            if s < len(CHAIN):
+                side, pair = CHAIN[s]
+                for i in (2 * pair, 2 * pair + 1):
+                    transpose(side, i)
+                for i in (2 * pair, 2 * pair + 1):
+                    collect(side, i)
+            if s + 1 < len(CHAIN) and CHAIN[s + 1][0] == "q":
+                pair = CHAIN[s + 1][1]
+                for i in (2 * pair, 2 * pair + 1):
+                    widen(i)
+            if s in job_in_front:
+                job_in_front[s]()
+            if 0 <= s - 1 < len(CHAIN):
+                quantize_first(*CHAIN[s - 1])
+            if 0 <= s - FIRST_PIECE_STEP < len(PIECES):
+                begin_piece(*PIECES[s - FIRST_PIECE_STEP])
+            if 0 <= s - FIRST_PIECE_STEP - 1 < len(PIECES):
+                finish_piece(*PIECES[s - FIRST_PIECE_STEP - 1])
+            if 0 <= s - 2 < len(CHAIN):
+                side, pair = CHAIN[s - 2]
+                if s - 2 == CHAIN.index(("q", 0)):
+                    spread_heads()
+                for i in (2 * pair, 2 * pair + 1):
+                    project(side, i)
+                for i in (2 * pair, 2 * pair + 1):
+                    round_projection(side, i)
+            if s in job_behind:
+                job_behind[s]()
+            if 0 <= s - 3 < len(CHAIN):
+                quantize_second(*CHAIN[s - 3])

@@ -26,9 +26,12 @@ P = 128
 PACK = 4
 HALF = 512
 TILES = N_FEAT // P
-CHAIN = [(side, pair) for pair in range(TILES // 2) for side in ("k", "q")]
-PIECES = [(i, j) for j in range(2) for i in range(TILES)]
-FIRST_PIECE_STEP = 6
+PROJECTIONS = [(side, 4 * half + n) for half in range(2) for side in ("k", "q") for n in range(4)]
+PIECES = [(i, j) for j in range(2) for i in range(4)] + [(i, j) for i in range(4, TILES) for j in range(2)]
+QUANTIZE_LAG = 2
+ROUND_LAG = 2
+FIRST_PIECE = 10
+FINISH_LAG = 1
 
 
 def tile_featurepairqkscoreattribution_d2p_kernel(
@@ -43,9 +46,10 @@ def tile_featurepairqkscoreattribution_d2p_kernel(
 
         ident = keep.tile([P, P], F32, name="ident")
         dk_in = [keep.tile([P, WIDTH], BF16, name="dk_in%d" % i) for i in range(TILES)]
-        dq_in = [keep.tile([P, 2, WIDTH], U8, name="dq_in%d" % s) for s in range(TILES // 2)]
+        dq_in = {}
         dq_sc = keep.tile([P, 64], F32, name="dq_sc")
         aq_in = [keep.tile([P, PACK, HALF], BF16, name="aq_in%d" % h) for h in range(2)]
+        wide_plain = set()
         ak_in = [keep.tile([P, PACK, HALF], BF16, name="ak_in%d" % h) for h in range(2)]
         g_in = keep.tile([P, PACK], BF16, name="g_in")
         head_in = keep.tile([P, HEADS], BF16, name="head_in")
@@ -68,9 +72,12 @@ def tile_featurepairqkscoreattribution_d2p_kernel(
         def load_dk(i):
             nc.sync.dma_start(out=dk_in[i][:], in_=dk[P * i : P * i + P, :])
 
-        def load_dq(s):
-            rows = dq_bytes[2 * P * s : 2 * P * s + 2 * P, :]
-            nc.sync.dma_start(out=dq_in[s][:], in_=rows.rearrange("(a p) k -> p a k", p=P))
+        def load_dq(first, count):
+            t = keep.tile([P, count, WIDTH], U8, name="dq_in%d" % first)
+            rows = dq_bytes[P * first : P * (first + count), :]
+            nc.sync.dma_start(out=t[:], in_=rows.rearrange("(a p) k -> p a k", p=P))
+            for n in range(count):
+                dq_in[first + n] = t[:, n, :]
 
         def load_tokens(dst, src, h):
             cols = src[:, HALF * h : HALF * h + HALF]
@@ -84,35 +91,33 @@ def tile_featurepairqkscoreattribution_d2p_kernel(
 
         def load_scales(queue, side, src):
             rows = src.bitcast(I32)
-            for quad in range(4):
+            for r in range(4):
                 queue.dma_start(
-                    out=scales_in[side][32 * quad : 32 * quad + 4, :].rearrange("r (g n) -> r g n", g=2),
-                    in_=rows[:, 4 * quad : 4 * quad + 4, :].rearrange("g r n -> r g n"),
+                    out=scales_in[side][r:P:32, :].rearrange("q (g n) -> q g n", g=2),
+                    in_=rows[:, r:16:4, :].rearrange("g q n -> q g n"),
                 )
 
-        load_dk(0)
-        load_dq(0)
         nc.scalar.dma_start(out=dq_sc[:], in_=dq_scale.rearrange("i j -> (i j)").partition_broadcast(P))
-        load_dk(1)
-        load_scales(nc.scalar, "k", wk_scales)
+        load_dq(0, 1)
+        load_dq(1, 1)
+        load_dk(0)
+        for s in range(1, 4):
+            load_dq(2 * s, 2)
+            load_dk(2 * s - 1)
+            if s < 3:
+                load_dk(2 * s)
         load_words("k", wk_words)
-        load_dk(2)
-        load_dk(3)
-        load_dq(1)
-        load_words("q", wq_words)
-        load_scales(nc.sync, "q", wq_scales)
-        load_tokens(aq_in, aq, 0)
-        load_dk(4)
-        nc.sync.dma_start(out=g_in[:], in_=g.rearrange("(p t) -> p t", t=PACK))
-        nc.sync.dma_start(out=head_in[:], in_=head_w.partition_broadcast(P))
-        load_dk(5)
-        load_dq(2)
-        load_tokens(ak_in, ak, 0)
+        load_scales(nc.sync, "k", wk_scales)
         load_dk(6)
         load_dk(7)
-        load_dq(3)
-        load_tokens(aq_in, aq, 1)
+        nc.sync.dma_start(out=head_in[:], in_=head_w.partition_broadcast(P))
+        nc.sync.dma_start(out=g_in[:], in_=g.rearrange("(p t) -> p t", t=PACK))
+        load_tokens(ak_in, ak, 0)
+        load_tokens(aq_in, aq, 0)
+        load_words("q", wq_words)
+        load_scales(nc.sync, "q", wq_scales)
         load_tokens(ak_in, ak, 1)
+        load_tokens(aq_in, aq, 1)
 
         def order_channels(side):
             for dst, src, run in ((words, words_in, 4), (scales, scales_in, 2)):
@@ -124,8 +129,9 @@ def tile_featurepairqkscoreattribution_d2p_kernel(
         def spread_heads():
             for h in range(HEADS):
                 rows = slice(32 * h, 32 * h + 32)
-                nc.scalar.copy(out=head_col[rows, 0:1], in_=head_in[rows, h : h + 1])
+                nc.scalar.activation(out=head_col[rows, 0:1], in_=head_in[rows, h : h + 1], func=COPY)
 
+        place = {(side, i): (i, n, 2) for i in range(TILES) for n, side in enumerate(("k", "q"))}
         dq_wide, first_in, first_q, second_in, bank_of = {}, {}, {}, {}, {}
 
         def widen(i):
@@ -134,11 +140,18 @@ def tile_featurepairqkscoreattribution_d2p_kernel(
             for j in range(8):
                 nc.vector.tensor_scalar(
                     out=by_pass[:, j // 4, 32 * (j % 4) : 32 * (j % 4) + 32, :, :],
-                    in0=dq_in[i // 2][:, i % 2, P * j : P * j + P].bitcast(FP8),
+                    in0=dq_in[i][:, P * j : P * j + P].bitcast(FP8),
                     scalar1=dq_sc[:, 8 * i + j : 8 * i + j + 1],
                     scalar2=None,
                     op0=MULT,
                 )
+
+        def widen_scalar(i):
+            dq_wide[i] = work.tile([P, WIDTH], BF16, name="wide", bufs=8)
+            wide_plain.add(i)
+            for j in range(8):
+                nc.scalar.activation(out=dq_wide[i][:, P * j : P * j + P], in_=dq_in[i][:, P * j : P * j + P].bitcast(FP8),
+                                     func=COPY, scale=dq_sc[:, 8 * i + j : 8 * i + j + 1])
 
         def transpose(side, i):
             pairs = (dk_in[i] if side == "k" else dq_wide[i])[:].bitcast(F32)
@@ -146,7 +159,7 @@ def tile_featurepairqkscoreattribution_d2p_kernel(
             for gg in range(2):
                 for u in range(2):
                     at = P * (2 * gg + u)
-                    if side == "k":
+                    if side == "k" or i in wide_plain:
                         src = pairs[:, 2 * P * gg + u : 2 * P * gg + 2 * P : 2]
                     else:
                         src = pairs[:, at : at + P]
@@ -154,26 +167,29 @@ def tile_featurepairqkscoreattribution_d2p_kernel(
             bank_of[side, i] = bank
 
         def collect(side, i):
-            if (side, i // 2) not in first_in:
-                first_in[side, i // 2] = work.tile([P, 2048], BF16, name="first_in", bufs=4, align_bytes=64)
-            dst = first_in[side, i // 2][:, 1024 * (i % 2) : 1024 * (i % 2) + 1024]
+            s, n, size = place[side, i]
+            if s not in first_in:
+                first_in[s] = work.tile([P, 1024 * size], BF16, name="first_in", bufs=8, align_bytes=64)
+            dst = first_in[s][:, 1024 * n : 1024 * n + 1024]
             nc.scalar.copy(
                 out=dst.bitcast(F32).rearrange("p (g f u) -> p g f u", g=2, u=2),
                 in_=bank_of[side, i][:].rearrange("p (g u f) -> p g f u", g=2, u=2),
             )
 
-        def quantize_first(side, s):
-            codes = work.tile([P, 512], U32, name="codes1", bufs=6, align_bytes=64)
-            sc = work.tile([P, 512], U8, name="scales1", bufs=6, align_bytes=64)
-            nc.vector.quantize_mx(out=codes[:].bitcast(FP8X4), scales=sc[:], in_=first_in[side, s][:])
-            first_q[side, s] = (codes, sc)
+        def quantize_first(s):
+            w = first_in[s].shape[1] // 4
+            codes = work.tile([P, w], U32, name="codes1", bufs=8, align_bytes=64)
+            sc = work.tile([P, w], U8, name="scales1", bufs=8, align_bytes=64)
+            nc.vector.quantize_mx(out=codes[:].bitcast(FP8X4), scales=sc[:], in_=first_in[s][:])
+            first_q[s] = (codes, sc)
 
         def project(side, i):
-            codes, sc = first_q[side, i // 2]
+            s, n, size = place[side, i]
+            codes, sc = first_q[s]
             bank = psum.tile([P, HALF], F32, name="bank")
             for t in range(PACK):
                 for gg in range(2):
-                    at = P * (2 * (i % 2) + gg)
+                    at = P * (2 * n + gg)
                     nc.tensor.matmul_mx(
                         out=bank[:, P * t : P * t + P],
                         lhsT=words[side][:, 128 * t + 64 * gg : 128 * t + 64 * gg + 64].bitcast(FP4X4),
@@ -186,21 +202,20 @@ def tile_featurepairqkscoreattribution_d2p_kernel(
             bank_of[side, i] = bank
 
         def round_projection(side, i):
-            if (side, i // 2) not in second_in:
-                second_in[side, i // 2] = work.tile([P, 2, HALF], BF16, name="second_in", bufs=4, align_bytes=64)
-            dst = second_in[side, i // 2][:, i % 2, :].rearrange("p (f t) -> p f t", t=PACK)
+            second_in[side, i] = work.tile([P, HALF], BF16, name="second_in", bufs=6, align_bytes=64)
+            dst = second_in[side, i][:].rearrange("p (f t) -> p f t", t=PACK)
             src = bank_of[side, i][:].rearrange("p (t f) -> p f t", t=PACK)
             if side == "k":
                 nc.scalar.copy(out=dst, in_=src)
             else:
                 nc.scalar.activation(out=dst, in_=src, func=COPY, scale=head_col[:, 0:1])
 
-        def quantize_second(side, s):
-            cols = slice(2 * P * s, 2 * P * s + 2 * P)
+        def quantize_second(side, i):
+            cols = slice(P * i, P * i + P)
             nc.vector.quantize_mx(
                 out=codes2[side][:, cols].bitcast(FP8X4),
                 scales=scales2[side][:, cols],
-                in_=second_in[side, s][:].rearrange("p a c -> p (a c)"),
+                in_=second_in[side, i][:],
             )
 
         ak_g, side_by_side = {}, {}
@@ -247,7 +262,7 @@ def tile_featurepairqkscoreattribution_d2p_kernel(
 
         def begin_piece(i, j):
             bank = product("aq", "ak", i, j)
-            c_part[i, j] = work.tile([P, HALF], F32, name="c_part", bufs=8)
+            c_part[i, j] = work.tile([P, HALF], F32, name="c_part", bufs=12)
             nc.scalar.activation(out=c_part[i, j][:], in_=bank[:], func=COPY, scale=divisor)
 
         def finish_piece(i, j):
@@ -257,55 +272,52 @@ def tile_featurepairqkscoreattribution_d2p_kernel(
             nc.sync.dma_start(out=out[P * i : P * i + P, HALF * j : HALF * j + HALF], in_=piece[:])
 
         on_vector, on_scalar = nc.vector.tensor_copy, nc.scalar.copy
-        job_in_front = {
-            1: lambda: order_channels("k"),
-            2: lambda: order_channels("q"),
-            3: lambda: interleave("aq", 0, 1, on_vector),
-            4: lambda: multiply_g(0),
-            5: lambda: interleave("ak", 0, 1, on_vector),
-            7: lambda: interleave("aq", 1, 1, on_vector),
-            8: lambda: multiply_g(1),
-            9: lambda: interleave("ak", 1, 1, on_vector),
-        }
-        job_behind = {
-            2: lambda: interleave("aq", 0, 0, on_scalar),
-            3: lambda: quantize_tokens("aq", 0),
-            4: lambda: interleave("ak", 0, 0, on_vector),
-            5: lambda: quantize_tokens("ak", 0),
-            6: lambda: interleave("aq", 1, 0, on_scalar),
-            7: lambda: quantize_tokens("aq", 1),
-            8: lambda: interleave("ak", 1, 0, on_vector),
-            9: lambda: quantize_tokens("ak", 1),
-        }
 
-        for s in range(FIRST_PIECE_STEP + len(PIECES) + 1):
-            if s < len(CHAIN):
-                side, pair = CHAIN[s]
-                for i in (2 * pair, 2 * pair + 1):
-                    transpose(side, i)
-                for i in (2 * pair, 2 * pair + 1):
-                    collect(side, i)
-            if s + 1 < len(CHAIN) and CHAIN[s + 1][0] == "q":
-                pair = CHAIN[s + 1][1]
-                for i in (2 * pair, 2 * pair + 1):
-                    widen(i)
-            if s in job_in_front:
-                job_in_front[s]()
-            if 0 <= s - 1 < len(CHAIN):
-                quantize_first(*CHAIN[s - 1])
-            if 0 <= s - FIRST_PIECE_STEP < len(PIECES):
-                begin_piece(*PIECES[s - FIRST_PIECE_STEP])
-            if 0 <= s - FIRST_PIECE_STEP - 1 < len(PIECES):
-                finish_piece(*PIECES[s - FIRST_PIECE_STEP - 1])
-            if 0 <= s - 2 < len(CHAIN):
-                side, pair = CHAIN[s - 2]
-                if s - 2 == CHAIN.index(("q", 0)):
-                    spread_heads()
-                for i in (2 * pair, 2 * pair + 1):
-                    project(side, i)
-                for i in (2 * pair, 2 * pair + 1):
-                    round_projection(side, i)
-            if s in job_behind:
-                job_behind[s]()
-            if 0 <= s - 3 < len(CHAIN):
-                quantize_second(*CHAIN[s - 3])
+        widen(0)
+        widen_scalar(1)
+        for i in range(TILES):
+            for side in ("k", "q"):
+                transpose(side, i)
+            for side in ("k", "q"):
+                collect(side, i)
+            if i + 2 < TILES:
+                widen(i + 2)
+            if i + 2 == TILES - 1:
+                order_channels("k")
+            elif QUANTIZE_LAG <= i < TILES - 1:
+                quantize_first(len(first_q))
+        spread_heads()
+        interleave("aq", 0, 0, on_scalar)
+
+        token_jobs = [
+            lambda: multiply_g(0),
+            lambda: interleave("ak", 0, 0, on_vector),
+            lambda: interleave("ak", 0, 1, on_vector),
+            lambda: interleave("aq", 0, 1, on_vector),
+            lambda: quantize_tokens("ak", 0),
+            lambda: quantize_tokens("aq", 0),
+            lambda: multiply_g(1),
+            lambda: interleave("ak", 1, 0, on_vector),
+            lambda: interleave("ak", 1, 1, on_vector),
+            lambda: interleave("aq", 1, 0, on_vector),
+            lambda: quantize_tokens("ak", 1),
+            lambda: interleave("aq", 1, 1, on_vector),
+            lambda: None,
+            lambda: quantize_tokens("aq", 1),
+        ]
+        for n in range(FIRST_PIECE + FINISH_LAG + len(PIECES)):
+            if n < len(PROJECTIONS):
+                project(*PROJECTIONS[n])
+                round_projection(*PROJECTIONS[n])
+            if 0 <= n - FIRST_PIECE < len(PIECES):
+                begin_piece(*PIECES[n - FIRST_PIECE])
+            if n % 2 == 0 and len(first_q) < TILES:
+                quantize_first(len(first_q))
+            if n == 2:
+                order_channels("q")
+            if n < len(token_jobs):
+                token_jobs[n]()
+            if 0 <= n - ROUND_LAG < len(PROJECTIONS):
+                quantize_second(*PROJECTIONS[n - ROUND_LAG])
+            if 0 <= n - FIRST_PIECE - FINISH_LAG:
+                finish_piece(*PIECES[n - FIRST_PIECE - FINISH_LAG])

@@ -47,12 +47,13 @@ def tile_featurepairqkscoreattribution_d2p_kernel(
         ident = keep.tile([P, P], F32, name="ident")
         dk_in = [keep.tile([P, WIDTH], BF16, name="dk_in%d" % i) for i in range(TILES)]
         dq_in = {}
+        scale_rows = keep.tile([P, 1], F32, name="scale_rows")
+        head_rows = keep.tile([P, 1], F32, name="head_rows")
         dq_sc = keep.tile([P, 64], F32, name="dq_sc")
         aq_in = [keep.tile([P, PACK, HALF], BF16, name="aq_in%d" % h) for h in range(2)]
         wide_plain = set()
         ak_in = [keep.tile([P, PACK, HALF], BF16, name="ak_in%d" % h) for h in range(2)]
         g_in = keep.tile([P, PACK], BF16, name="g_in")
-        head_in = keep.tile([P, HEADS], BF16, name="head_in")
         head_col = keep.tile([P, 1], F32, name="head_col")
         words_in, words, scales_in, scales = {}, {}, {}, {}
         for side in ("k", "q"):
@@ -65,7 +66,9 @@ def tile_featurepairqkscoreattribution_d2p_kernel(
             codes2[name] = keep.tile([P, N_FEAT], U32, name="codes2_" + name, align_bytes=64)
             scales2[name] = keep.tile([P, N_FEAT], U8, name="scales2_" + name, align_bytes=64)
 
-        for side in ("k", "q"):
+        nc.vector.memset(scale_rows[64:P, :], 0.0)
+        nc.vector.memset(head_rows[:], 0.0)
+        for side in ("q", "k"):
             nc.vector.memset(scales_in[side][:], 0)
         make_identity(nc, ident[:])
 
@@ -97,7 +100,7 @@ def tile_featurepairqkscoreattribution_d2p_kernel(
                     in_=rows[:, r:16:4, :].rearrange("g q n -> q g n"),
                 )
 
-        nc.scalar.dma_start(out=dq_sc[:], in_=dq_scale.rearrange("i j -> (i j)").partition_broadcast(P))
+        nc.scalar.dma_start(out=scale_rows[0:64, :], in_=dq_scale.rearrange("i (j o) -> (i j) o", o=1))
         load_dq(0, 1)
         load_dq(1, 1)
         load_dk(0)
@@ -110,7 +113,7 @@ def tile_featurepairqkscoreattribution_d2p_kernel(
         load_scales(nc.sync, "k", wk_scales)
         load_dk(6)
         load_dk(7)
-        nc.sync.dma_start(out=head_in[:], in_=head_w.partition_broadcast(P))
+        nc.sync.dma_start(out=head_rows[0:2, :], in_=head_w.bitcast(F32).rearrange("(w o) -> w o", o=1))
         nc.sync.dma_start(out=g_in[:], in_=g.rearrange("(p t) -> p t", t=PACK))
         load_tokens(ak_in, ak, 0)
         load_tokens(aq_in, aq, 0)
@@ -126,7 +129,16 @@ def tile_featurepairqkscoreattribution_d2p_kernel(
                     in_=src[side][:].rearrange("p (x t w) -> p t x w", t=4, w=run),
                 )
 
+        def along_partitions(rows):
+            bank = psum.tile([P, HALF], F32, name="bank")
+            nc.tensor.transpose(bank[:, 0:P], rows[:, 0:1].to_broadcast([P, P]), ident[:])
+            return bank
+
+        def spread_scales():
+            nc.vector.tensor_copy(out=dq_sc[:], in_=along_partitions(scale_rows)[:, 0:64])
+
         def spread_heads():
+            head_in = along_partitions(head_rows)[:, 0:2].bitcast(BF16)
             for h in range(HEADS):
                 rows = slice(32 * h, 32 * h + 32)
                 nc.scalar.activation(out=head_col[rows, 0:1], in_=head_in[rows, h : h + 1], func=COPY)
@@ -273,6 +285,7 @@ def tile_featurepairqkscoreattribution_d2p_kernel(
 
         on_vector, on_scalar = nc.vector.tensor_copy, nc.scalar.copy
 
+        spread_scales()
         widen(0)
         widen_scalar(1)
         for i in range(TILES):

@@ -26,12 +26,11 @@ P = 128
 PACK = 4
 HALF = 512
 TILES = N_FEAT // P
-PROJECTIONS = [(side, 4 * half + n) for half in range(2) for side in ("k", "q") for n in range(4)]
+PROJECTIONS = [("k", 0), ("k", 1), ("k", 2), ("k", 3), ("q", 0), ("q", 1), ("q", 2), ("q", 3), ("k", 4), ("k", 5), ("k", 6), ("k", 7), ("q", 4), ("q", 5), ("q", 6), ("q", 7)]
 PIECES = [(i, j) for j in range(2) for i in range(4)] + [(i, j) for i in range(4, TILES) for j in range(2)]
-QUANTIZE_LAG = 2
-ROUND_LAG = 2
-FIRST_PIECE = 10
-FINISH_LAG = 1
+ROUND_LAG = 3
+FIRST_PIECE = 8
+FINISH_LAG = 2
 
 
 def tile_featurepairqkscoreattribution_d2p_kernel(
@@ -51,10 +50,11 @@ def tile_featurepairqkscoreattribution_d2p_kernel(
         head_rows = keep.tile([P, 1], F32, name="head_rows")
         dq_sc = keep.tile([P, 64], F32, name="dq_sc")
         aq_in = [keep.tile([P, PACK, HALF], BF16, name="aq_in%d" % h) for h in range(2)]
-        wide_plain = set()
+        wide_plain, unscaled = set(), set()
         ak_in = [keep.tile([P, PACK, HALF], BF16, name="ak_in%d" % h) for h in range(2)]
         g_in = keep.tile([P, PACK], BF16, name="g_in")
         head_col = keep.tile([P, 1], F32, name="head_col")
+        pass_sc = keep.tile([P, 2 * TILES], F32, name="pass_sc")
         words_in, words, scales_in, scales = {}, {}, {}, {}
         for side in ("k", "q"):
             words_in[side] = keep.tile([P, 512], I32, name="words_in_" + side, align_bytes=64)
@@ -101,25 +101,28 @@ def tile_featurepairqkscoreattribution_d2p_kernel(
                 )
 
         nc.scalar.dma_start(out=scale_rows[0:64, :], in_=dq_scale.rearrange("i (j o) -> (i j) o", o=1))
-        load_dq(0, 1)
-        load_dq(1, 1)
         load_dk(0)
-        for s in range(1, 4):
-            load_dq(2 * s, 2)
-            load_dk(2 * s - 1)
-            if s < 3:
-                load_dk(2 * s)
+        load_dq(1, 1)
+        load_dq(0, 1)
+        load_dq(2, 2)
+        load_dk(1)
+        load_dk(2)
+        load_dq(4, 2)
+        load_dk(3)
         load_words("k", wk_words)
         load_scales(nc.sync, "k", wk_scales)
-        load_dk(6)
-        load_dk(7)
-        nc.sync.dma_start(out=head_rows[0:2, :], in_=head_w.bitcast(F32).rearrange("(w o) -> w o", o=1))
-        nc.sync.dma_start(out=g_in[:], in_=g.rearrange("(p t) -> p t", t=PACK))
-        load_tokens(ak_in, ak, 0)
         load_tokens(aq_in, aq, 0)
+        load_dq(6, 2)
+        load_dk(4)
+        load_tokens(ak_in, ak, 0)
+        nc.sync.dma_start(out=g_in[:], in_=g.rearrange("(p t) -> p t", t=PACK))
         load_words("q", wq_words)
         load_scales(nc.sync, "q", wq_scales)
+        load_dk(5)
+        nc.sync.dma_start(out=head_rows[0:2, :], in_=head_w.bitcast(F32).rearrange("(w o) -> w o", o=1))
+        load_dk(6)
         load_tokens(ak_in, ak, 1)
+        load_dk(7)
         load_tokens(aq_in, aq, 1)
 
         def order_channels(side):
@@ -135,7 +138,12 @@ def tile_featurepairqkscoreattribution_d2p_kernel(
             return bank
 
         def spread_scales():
-            nc.vector.tensor_copy(out=dq_sc[:], in_=along_partitions(scale_rows)[:, 0:64])
+            bank = along_partitions(scale_rows)
+            nc.scalar.activation(out=dq_sc[:], in_=bank[:, 0:64], func=COPY)
+            by_quarter = bank[:, 0:64].rearrange("p (x q) -> p x q", q=4)
+            for q in range(4):
+                rows = slice(32 * q, 32 * q + 32)
+                nc.scalar.copy(out=pass_sc[rows, :], in_=by_quarter[rows, :, q])
 
         def spread_heads():
             head_in = along_partitions(head_rows)[:, 0:2].bitcast(BF16)
@@ -158,12 +166,11 @@ def tile_featurepairqkscoreattribution_d2p_kernel(
                     op0=MULT,
                 )
 
-        def widen_scalar(i):
+        def cast(i):
             dq_wide[i] = work.tile([P, WIDTH], BF16, name="wide", bufs=8)
             wide_plain.add(i)
-            for j in range(8):
-                nc.scalar.activation(out=dq_wide[i][:, P * j : P * j + P], in_=dq_in[i][:, P * j : P * j + P].bitcast(FP8),
-                                     func=COPY, scale=dq_sc[:, 8 * i + j : 8 * i + j + 1])
+            unscaled.add(i)
+            nc.scalar.copy(out=dq_wide[i][:], in_=dq_in[i].bitcast(FP8))
 
         def transpose(side, i):
             pairs = (dk_in[i] if side == "k" else dq_wide[i])[:].bitcast(F32)
@@ -183,6 +190,14 @@ def tile_featurepairqkscoreattribution_d2p_kernel(
             if s not in first_in:
                 first_in[s] = work.tile([P, 1024 * size], BF16, name="first_in", bufs=8, align_bytes=64)
             dst = first_in[s][:, 1024 * n : 1024 * n + 1024]
+            if side == "q" and i in unscaled:
+                by_pass = dst.rearrange("p (g f u e) -> p g f u e", g=2, u=2, e=2)
+                src = bank_of[side, i][:].bitcast(BF16).rearrange("p (g u f e) -> p g f u e", g=2, u=2, e=2)
+                for gg in range(2):
+                    nc.vector.tensor_scalar(
+                        out=by_pass[:, gg], in0=src[:, gg], scalar1=pass_sc[:, 2 * i + gg : 2 * i + gg + 1], scalar2=None, op0=MULT
+                    )
+                return
             nc.scalar.copy(
                 out=dst.bitcast(F32).rearrange("p (g f u) -> p g f u", g=2, u=2),
                 in_=bank_of[side, i][:].rearrange("p (g u f) -> p g f u", g=2, u=2),
@@ -214,8 +229,9 @@ def tile_featurepairqkscoreattribution_d2p_kernel(
             bank_of[side, i] = bank
 
         def round_projection(side, i):
-            second_in[side, i] = work.tile([P, HALF], BF16, name="second_in", bufs=6, align_bytes=64)
-            dst = second_in[side, i][:].rearrange("p (f t) -> p f t", t=PACK)
+            if i % 2 == 0:
+                second_in[side, i // 2] = work.tile([P, 2 * HALF], BF16, name="second_in", bufs=4, align_bytes=64)
+            dst = second_in[side, i // 2][:, HALF * (i % 2) : HALF * (i % 2) + HALF].rearrange("p (f t) -> p f t", t=PACK)
             src = bank_of[side, i][:].rearrange("p (t f) -> p f t", t=PACK)
             if side == "k":
                 nc.scalar.copy(out=dst, in_=src)
@@ -223,7 +239,7 @@ def tile_featurepairqkscoreattribution_d2p_kernel(
                 nc.scalar.activation(out=dst, in_=src, func=COPY, scale=head_col[:, 0:1])
 
         def quantize_second(side, i):
-            cols = slice(P * i, P * i + P)
+            cols = slice(2 * P * i, 2 * P * i + 2 * P)
             nc.vector.quantize_mx(
                 out=codes2[side][:, cols].bitcast(FP8X4),
                 scales=scales2[side][:, cols],
@@ -277,60 +293,73 @@ def tile_featurepairqkscoreattribution_d2p_kernel(
             c_part[i, j] = work.tile([P, HALF], F32, name="c_part", bufs=12)
             nc.scalar.activation(out=c_part[i, j][:], in_=bank[:], func=COPY, scale=divisor)
 
-        def finish_piece(i, j):
-            bank = product("q", "k", i, j)
+        def multiply_piece(i, j):
+            bank_of["m", i, j] = product("q", "k", i, j)
+
+        def store_piece(i, j):
+            bank = bank_of["m", i, j]
             piece = work.tile([P, HALF], F32, name="piece", bufs=8)
             nc.vector.tensor_tensor(out=piece[:], in0=bank[:], in1=c_part[i, j][:], op=MULT)
             nc.sync.dma_start(out=out[P * i : P * i + P, HALF * j : HALF * j + HALF], in_=piece[:])
 
         on_vector, on_scalar = nc.vector.tensor_copy, nc.scalar.copy
 
-        spread_scales()
-        widen(0)
-        widen_scalar(1)
-        for i in range(TILES):
-            for side in ("k", "q"):
-                transpose(side, i)
-            for side in ("k", "q"):
+        def turn(side, i):
+            transpose(side, i)
+            if side == "k" or i not in unscaled:
                 collect(side, i)
-            if i + 2 < TILES:
-                widen(i + 2)
-            if i + 2 == TILES - 1:
-                order_channels("k")
-            elif QUANTIZE_LAG <= i < TILES - 1:
-                quantize_first(len(first_q))
-        spread_heads()
-        interleave("aq", 0, 0, on_scalar)
 
-        token_jobs = [
-            lambda: multiply_g(0),
-            lambda: interleave("ak", 0, 0, on_vector),
-            lambda: interleave("ak", 0, 1, on_vector),
-            lambda: interleave("aq", 0, 1, on_vector),
-            lambda: quantize_tokens("ak", 0),
-            lambda: quantize_tokens("aq", 0),
-            lambda: multiply_g(1),
-            lambda: interleave("ak", 1, 0, on_vector),
-            lambda: interleave("ak", 1, 1, on_vector),
-            lambda: interleave("aq", 1, 0, on_vector),
-            lambda: quantize_tokens("ak", 1),
-            lambda: interleave("aq", 1, 1, on_vector),
-            lambda: None,
-            lambda: quantize_tokens("aq", 1),
-        ]
-        for n in range(FIRST_PIECE + FINISH_LAG + len(PIECES)):
+        def turn_pair(i):
+            for side in ("k", "q"):
+                turn(side, i)
+
+        jobs = {
+            0: [lambda: widen(6), lambda: interleave("aq", 0, 1, on_scalar), lambda: quantize_first(3)],
+            1: [lambda: turn_pair(4), lambda: multiply_g(0), lambda: order_channels("q"), lambda: interleave("ak", 0, 0, on_vector)],
+            2: [lambda: quantize_tokens("aq", 0), lambda: interleave("ak", 0, 1, on_vector), lambda: cast(7), lambda: quantize_first(4)],
+            3: [lambda: turn_pair(5), lambda: spread_heads(), lambda: quantize_tokens("ak", 0), lambda: collect("q", 5)],
+            4: [lambda: multiply_g(1), lambda: quantize_first(5)],
+            5: [lambda: turn_pair(6), lambda: interleave("ak", 1, 0, on_vector)],
+            6: [lambda: interleave("ak", 1, 1, on_vector), lambda: quantize_first(6)],
+            7: [lambda: turn_pair(7), lambda: collect("q", 7)],
+            8: [lambda: quantize_tokens("ak", 1), lambda: quantize_first(7)],
+            10: [lambda: interleave("aq", 1, 0, on_vector)],
+            12: [lambda: interleave("aq", 1, 1, on_vector)],
+            14: [lambda: quantize_tokens("aq", 1)],
+        }
+
+        spread_scales()
+        cast(1)
+        widen(0)
+        turn("k", 0)
+        turn("q", 1)
+        cast(3)
+        widen(2)
+        turn("q", 0)
+        turn("k", 1)
+        collect("q", 1)
+        turn_pair(2)
+        widen(4)
+        quantize_first(0)
+        turn_pair(3)
+        quantize_first(1)
+        order_channels("k")
+        quantize_first(2)
+        collect("q", 3)
+        cast(5)
+        interleave("aq", 0, 0, on_scalar)
+        for n in range(FIRST_PIECE + FINISH_LAG + len(PIECES) + 1):
             if n < len(PROJECTIONS):
                 project(*PROJECTIONS[n])
                 round_projection(*PROJECTIONS[n])
             if 0 <= n - FIRST_PIECE < len(PIECES):
                 begin_piece(*PIECES[n - FIRST_PIECE])
-            if n % 2 == 0 and len(first_q) < TILES:
-                quantize_first(len(first_q))
-            if n == 2:
-                order_channels("q")
-            if n < len(token_jobs):
-                token_jobs[n]()
-            if 0 <= n - ROUND_LAG < len(PROJECTIONS):
-                quantize_second(*PROJECTIONS[n - ROUND_LAG])
-            if 0 <= n - FIRST_PIECE - FINISH_LAG:
-                finish_piece(*PIECES[n - FIRST_PIECE - FINISH_LAG])
+            if 0 <= n - ROUND_LAG < len(PROJECTIONS) and (n - ROUND_LAG) % 2 == 1:
+                side, i = PROJECTIONS[n - ROUND_LAG]
+                quantize_second(side, i // 2)
+            if 0 <= n - FIRST_PIECE - FINISH_LAG < len(PIECES):
+                multiply_piece(*PIECES[n - FIRST_PIECE - FINISH_LAG])
+            for job in jobs.get(n, []):
+                job()
+            if 0 <= n - FIRST_PIECE - FINISH_LAG - 1 < len(PIECES):
+                store_piece(*PIECES[n - FIRST_PIECE - FINISH_LAG - 1])

@@ -26,11 +26,16 @@ P = 128
 PACK = 4
 HALF = 512
 TILES = N_FEAT // P
-PROJECTIONS = [("k", 0), ("k", 1), ("k", 2), ("k", 3), ("q", 0), ("q", 1), ("q", 2), ("q", 3), ("k", 4), ("k", 5), ("k", 6), ("k", 7), ("q", 4), ("q", 5), ("q", 6), ("q", 7)]
+PROJECTIONS = (
+    [(side, i) for side in ("k", "q") for i in range(4)]
+    + [("k", i) for i in range(4, TILES)]
+    + [("q", 4), ("q", 5), None, ("q", 6), None, ("q", 7)]
+)
 PIECES = [(i, j) for j in range(2) for i in range(4)] + [(i, j) for i in range(4, TILES) for j in range(2)]
-ROUND_LAG = 3
+ROUND_LAG = 2
 FIRST_PIECE = 8
-FINISH_LAG = 2
+PER_TURN = 2
+AHEAD = 3
 
 
 def tile_featurepairqkscoreattribution_d2p_kernel(
@@ -50,11 +55,9 @@ def tile_featurepairqkscoreattribution_d2p_kernel(
         head_rows = keep.tile([P, 1], F32, name="head_rows")
         dq_sc = keep.tile([P, 64], F32, name="dq_sc")
         aq_in = [keep.tile([P, PACK, HALF], BF16, name="aq_in%d" % h) for h in range(2)]
-        wide_plain, unscaled = set(), set()
         ak_in = [keep.tile([P, PACK, HALF], BF16, name="ak_in%d" % h) for h in range(2)]
         g_in = keep.tile([P, PACK], BF16, name="g_in")
         head_col = keep.tile([P, 1], F32, name="head_col")
-        pass_sc = keep.tile([P, 2 * TILES], F32, name="pass_sc")
         words_in, words, scales_in, scales = {}, {}, {}, {}
         for side in ("k", "q"):
             words_in[side] = keep.tile([P, 512], I32, name="words_in_" + side, align_bytes=64)
@@ -66,8 +69,8 @@ def tile_featurepairqkscoreattribution_d2p_kernel(
             codes2[name] = keep.tile([P, N_FEAT], U32, name="codes2_" + name, align_bytes=64)
             scales2[name] = keep.tile([P, N_FEAT], U8, name="scales2_" + name, align_bytes=64)
 
-        nc.vector.memset(scale_rows[64:P, :], 0.0)
         nc.vector.memset(head_rows[:], 0.0)
+        nc.vector.memset(scale_rows[64:P, :], 0.0)
         for side in ("q", "k"):
             nc.vector.memset(scales_in[side][:], 0)
         make_identity(nc, ident[:])
@@ -92,34 +95,34 @@ def tile_featurepairqkscoreattribution_d2p_kernel(
                 in_=src.bitcast(I32).rearrange("g p n -> p g n"),
             )
 
-        def load_scales(queue, side, src):
+        def load_scales(side, src):
             rows = src.bitcast(I32)
             for r in range(4):
-                queue.dma_start(
+                nc.sync.dma_start(
                     out=scales_in[side][r:P:32, :].rearrange("q (g n) -> q g n", g=2),
                     in_=rows[:, r:16:4, :].rearrange("g q n -> q g n"),
                 )
 
         nc.scalar.dma_start(out=scale_rows[0:64, :], in_=dq_scale.rearrange("i (j o) -> (i j) o", o=1))
-        load_dk(0)
-        load_dq(1, 1)
         load_dq(0, 1)
+        load_dq(1, 1)
+        load_dk(0)
         load_dq(2, 2)
         load_dk(1)
         load_dk(2)
         load_dq(4, 2)
+        nc.sync.dma_start(out=head_rows[0:2, :], in_=head_w.bitcast(F32).rearrange("(w o) -> w o", o=1))
         load_dk(3)
         load_words("k", wk_words)
-        load_scales(nc.sync, "k", wk_scales)
-        load_tokens(aq_in, aq, 0)
+        load_scales("k", wk_scales)
         load_dq(6, 2)
+        load_tokens(aq_in, aq, 0)
         load_dk(4)
+        load_words("q", wq_words)
+        load_scales("q", wq_scales)
         load_tokens(ak_in, ak, 0)
         nc.sync.dma_start(out=g_in[:], in_=g.rearrange("(p t) -> p t", t=PACK))
-        load_words("q", wq_words)
-        load_scales(nc.sync, "q", wq_scales)
         load_dk(5)
-        nc.sync.dma_start(out=head_rows[0:2, :], in_=head_w.bitcast(F32).rearrange("(w o) -> w o", o=1))
         load_dk(6)
         load_tokens(ak_in, ak, 1)
         load_dk(7)
@@ -138,12 +141,7 @@ def tile_featurepairqkscoreattribution_d2p_kernel(
             return bank
 
         def spread_scales():
-            bank = along_partitions(scale_rows)
-            nc.scalar.activation(out=dq_sc[:], in_=bank[:, 0:64], func=COPY)
-            by_quarter = bank[:, 0:64].rearrange("p (x q) -> p x q", q=4)
-            for q in range(4):
-                rows = slice(32 * q, 32 * q + 32)
-                nc.scalar.copy(out=pass_sc[rows, :], in_=by_quarter[rows, :, q])
+            nc.scalar.activation(out=dq_sc[:], in_=along_partitions(scale_rows)[:, 0:64], func=COPY)
 
         def spread_heads():
             head_in = along_partitions(head_rows)[:, 0:2].bitcast(BF16)
@@ -151,8 +149,10 @@ def tile_featurepairqkscoreattribution_d2p_kernel(
                 rows = slice(32 * h, 32 * h + 32)
                 nc.scalar.activation(out=head_col[rows, 0:1], in_=head_in[rows, h : h + 1], func=COPY)
 
-        place = {(side, i): (i, n, 2) for i in range(TILES) for n, side in enumerate(("k", "q"))}
         dq_wide, first_in, first_q, second_in, bank_of = {}, {}, {}, {}, {}
+        in_order_of_k = set()
+        quantized = set()
+        slot = {"k": 0, "q": 1}
 
         def widen(i):
             dq_wide[i] = work.tile([P, WIDTH], BF16, name="wide", bufs=8)
@@ -166,57 +166,52 @@ def tile_featurepairqkscoreattribution_d2p_kernel(
                     op0=MULT,
                 )
 
-        def cast(i):
+        def widen_on_scalar(i):
             dq_wide[i] = work.tile([P, WIDTH], BF16, name="wide", bufs=8)
-            wide_plain.add(i)
-            unscaled.add(i)
-            nc.scalar.copy(out=dq_wide[i][:], in_=dq_in[i].bitcast(FP8))
+            in_order_of_k.add(i)
+            for j in range(8):
+                nc.scalar.activation(
+                    out=dq_wide[i][:, P * j : P * j + P],
+                    in_=dq_in[i][:, P * j : P * j + P].bitcast(FP8),
+                    func=COPY,
+                    scale=dq_sc[:, 8 * i + j : 8 * i + j + 1],
+                )
 
-        def transpose(side, i):
+        def turn(side, i):
             pairs = (dk_in[i] if side == "k" else dq_wide[i])[:].bitcast(F32)
             bank = psum.tile([P, HALF], F32, name="bank")
             for gg in range(2):
                 for u in range(2):
                     at = P * (2 * gg + u)
-                    if side == "k" or i in wide_plain:
+                    if side == "k" or i in in_order_of_k:
                         src = pairs[:, 2 * P * gg + u : 2 * P * gg + 2 * P : 2]
                     else:
                         src = pairs[:, at : at + P]
                     nc.tensor.transpose(bank[:, at : at + P], src, ident[:])
-            bank_of[side, i] = bank
-
-        def collect(side, i):
-            s, n, size = place[side, i]
-            if s not in first_in:
-                first_in[s] = work.tile([P, 1024 * size], BF16, name="first_in", bufs=8, align_bytes=64)
-            dst = first_in[s][:, 1024 * n : 1024 * n + 1024]
-            if side == "q" and i in unscaled:
-                by_pass = dst.rearrange("p (g f u e) -> p g f u e", g=2, u=2, e=2)
-                src = bank_of[side, i][:].bitcast(BF16).rearrange("p (g u f e) -> p g f u e", g=2, u=2, e=2)
-                for gg in range(2):
-                    nc.vector.tensor_scalar(
-                        out=by_pass[:, gg], in0=src[:, gg], scalar1=pass_sc[:, 2 * i + gg : 2 * i + gg + 1], scalar2=None, op0=MULT
-                    )
-                return
+            if i not in first_in:
+                first_in[i] = work.tile([P, 2 * WIDTH], BF16, name="first_in", bufs=8, align_bytes=64)
+            dst = first_in[i][:, WIDTH * slot[side] : WIDTH * slot[side] + WIDTH]
             nc.scalar.copy(
                 out=dst.bitcast(F32).rearrange("p (g f u) -> p g f u", g=2, u=2),
-                in_=bank_of[side, i][:].rearrange("p (g u f) -> p g f u", g=2, u=2),
+                in_=bank[:].rearrange("p (g u f) -> p g f u", g=2, u=2),
             )
 
-        def quantize_first(s):
-            w = first_in[s].shape[1] // 4
-            codes = work.tile([P, w], U32, name="codes1", bufs=8, align_bytes=64)
-            sc = work.tile([P, w], U8, name="scales1", bufs=8, align_bytes=64)
-            nc.vector.quantize_mx(out=codes[:].bitcast(FP8X4), scales=sc[:], in_=first_in[s][:])
-            first_q[s] = (codes, sc)
+        def turn_pair(i):
+            turn("k", i)
+            turn("q", i)
+
+        def quantize_first(i):
+            codes = work.tile([P, HALF], U32, name="codes1", bufs=8, align_bytes=64)
+            sc = work.tile([P, HALF], U8, name="scales1", bufs=8, align_bytes=64)
+            nc.vector.quantize_mx(out=codes[:].bitcast(FP8X4), scales=sc[:], in_=first_in[i][:])
+            first_q[i] = (codes, sc)
 
         def project(side, i):
-            s, n, size = place[side, i]
-            codes, sc = first_q[s]
+            codes, sc = first_q[i]
             bank = psum.tile([P, HALF], F32, name="bank")
             for t in range(PACK):
                 for gg in range(2):
-                    at = P * (2 * n + gg)
+                    at = P * (2 * slot[side] + gg)
                     nc.tensor.matmul_mx(
                         out=bank[:, P * t : P * t + P],
                         lhsT=words[side][:, 128 * t + 64 * gg : 128 * t + 64 * gg + 64].bitcast(FP4X4),
@@ -226,24 +221,23 @@ def tile_featurepairqkscoreattribution_d2p_kernel(
                         start=(gg == 0),
                         stop=(gg == 1),
                     )
-            bank_of[side, i] = bank
-
-        def round_projection(side, i):
             if i % 2 == 0:
                 second_in[side, i // 2] = work.tile([P, 2 * HALF], BF16, name="second_in", bufs=4, align_bytes=64)
             dst = second_in[side, i // 2][:, HALF * (i % 2) : HALF * (i % 2) + HALF].rearrange("p (f t) -> p f t", t=PACK)
-            src = bank_of[side, i][:].rearrange("p (t f) -> p f t", t=PACK)
+            src = bank[:].rearrange("p (t f) -> p f t", t=PACK)
             if side == "k":
                 nc.scalar.copy(out=dst, in_=src)
             else:
                 nc.scalar.activation(out=dst, in_=src, func=COPY, scale=head_col[:, 0:1])
 
-        def quantize_second(side, i):
-            cols = slice(2 * P * i, 2 * P * i + 2 * P)
+        def quantize_second(side, first, count):
+            quantized.update((side, i) for i in range(first, first + count))
+            cols = slice(P * first, P * (first + count))
+            at = HALF * (first % 2)
             nc.vector.quantize_mx(
                 out=codes2[side][:, cols].bitcast(FP8X4),
                 scales=scales2[side][:, cols],
-                in_=second_in[side, i][:],
+                in_=second_in[side, first // 2][:, at : at + HALF * count],
             )
 
         ak_g, side_by_side = {}, {}
@@ -255,21 +249,26 @@ def tile_featurepairqkscoreattribution_d2p_kernel(
                     out=ak_g[h][:, t, :], in0=ak_in[h][:, t, :], scalar1=g_in[:, t : t + 1], scalar2=None, op0=MULT
                 )
 
-        def interleave(name, h, part, copy):
+        def interleave(name, first, count, copy):
+            h, at = first // 4, P * (first % 4)
             if (name, h) not in side_by_side:
-                side_by_side[name, h] = work.tile([P, 2048], BF16, name="side_by_side", bufs=4, align_bytes=64)
+                side_by_side[name, h] = work.tile([P, PACK * HALF], BF16, name="side_by_side", bufs=4, align_bytes=64)
             src = aq_in[h] if name == "aq" else ak_g[h]
             copy(
-                out=side_by_side[name, h][:, 1024 * part : 1024 * part + 1024].rearrange(
+                out=side_by_side[name, h][:, PACK * at : PACK * (at + P * count)].rearrange(
                     "p (c i t) -> p c t i", i=4, t=PACK
                 ),
-                in_=src[:, :, 256 * part : 256 * part + 256].rearrange("p t (c i) -> p c t i", i=4),
+                in_=src[:, :, at : at + P * count].rearrange("p t (c i) -> p c t i", i=4),
             )
 
-        def quantize_tokens(name, h):
-            cols = slice(HALF * h, HALF * h + HALF)
+        def quantize_tokens(name, first, count):
+            quantized.update((name, i) for i in range(first, first + count))
+            cols = slice(P * first, P * (first + count))
+            at = HALF * (first % 4)
             nc.vector.quantize_mx(
-                out=codes2[name][:, cols].bitcast(FP8X4), scales=scales2[name][:, cols], in_=side_by_side[name, h][:]
+                out=codes2[name][:, cols].bitcast(FP8X4),
+                scales=scales2[name][:, cols],
+                in_=side_by_side[name, first // 4][:, at : at + HALF * count],
             )
 
         divisor = 1.0 / (TOKENS * math.sqrt(CHANNELS // HEADS))
@@ -304,62 +303,69 @@ def tile_featurepairqkscoreattribution_d2p_kernel(
 
         on_vector, on_scalar = nc.vector.tensor_copy, nc.scalar.copy
 
-        def turn(side, i):
-            transpose(side, i)
-            if side == "k" or i not in unscaled:
-                collect(side, i)
-
-        def turn_pair(i):
-            for side in ("k", "q"):
-                turn(side, i)
-
-        jobs = {
-            0: [lambda: widen(6), lambda: interleave("aq", 0, 1, on_scalar), lambda: quantize_first(3)],
-            1: [lambda: turn_pair(4), lambda: multiply_g(0), lambda: order_channels("q"), lambda: interleave("ak", 0, 0, on_vector)],
-            2: [lambda: quantize_tokens("aq", 0), lambda: interleave("ak", 0, 1, on_vector), lambda: cast(7), lambda: quantize_first(4)],
-            3: [lambda: turn_pair(5), lambda: spread_heads(), lambda: quantize_tokens("ak", 0), lambda: collect("q", 5)],
-            4: [lambda: multiply_g(1), lambda: quantize_first(5)],
-            5: [lambda: turn_pair(6), lambda: interleave("ak", 1, 0, on_vector)],
-            6: [lambda: interleave("ak", 1, 1, on_vector), lambda: quantize_first(6)],
-            7: [lambda: turn_pair(7), lambda: collect("q", 7)],
-            8: [lambda: quantize_tokens("ak", 1), lambda: quantize_first(7)],
-            10: [lambda: interleave("aq", 1, 0, on_vector)],
-            12: [lambda: interleave("aq", 1, 1, on_vector)],
-            14: [lambda: quantize_tokens("aq", 1)],
-        }
-
         spread_scales()
-        cast(1)
         widen(0)
-        turn("k", 0)
-        turn("q", 1)
-        cast(3)
+        widen_on_scalar(1)
+        turn_pair(0)
         widen(2)
-        turn("q", 0)
-        turn("k", 1)
-        collect("q", 1)
+        turn_pair(1)
+        widen(3)
         turn_pair(2)
         widen(4)
         quantize_first(0)
         turn_pair(3)
+        spread_heads()
         quantize_first(1)
         order_channels("k")
+        widen(5)
         quantize_first(2)
-        collect("q", 3)
-        cast(5)
-        interleave("aq", 0, 0, on_scalar)
-        for n in range(FIRST_PIECE + FINISH_LAG + len(PIECES) + 1):
-            if n < len(PROJECTIONS):
+        interleave("aq", 0, 2, on_scalar)
+
+        jobs = {
+            0: [(widen, 6), (quantize_first, 3), (widen, 7), (interleave, "aq", 2, 1, on_scalar)],
+            1: [(turn_pair, 4), (order_channels, "q"), (multiply_g, 0), (interleave, "aq", 3, 1, on_vector)],
+            2: [
+                (interleave, "ak", 0, 2, on_vector),
+                (quantize_tokens, "aq", 0, 4),
+                (quantize_first, 4),
+                (interleave, "ak", 2, 2, on_vector),
+            ],
+            3: [(turn_pair, 5), (quantize_tokens, "ak", 0, 4)],
+            4: [(multiply_g, 1), (quantize_first, 5)],
+            5: [(turn_pair, 6), (interleave, "ak", 4, 2, on_vector)],
+            6: [(interleave, "ak", 6, 2, on_vector), (quantize_first, 6)],
+            7: [(turn_pair, 7)],
+            8: [(quantize_tokens, "ak", 4, 4), (quantize_first, 7)],
+            10: [(interleave, "aq", 4, 2, on_vector)],
+            12: [(quantize_tokens, "aq", 4, 2)],
+            13: [(interleave, "aq", 6, 2, on_vector)],
+            15: [(quantize_tokens, "aq", 6, 2)],
+        }
+
+        begun, multiplied, stored = {}, 0, 0
+        for n in range(len(PROJECTIONS) + len(PIECES)):
+            if n < len(PROJECTIONS) and PROJECTIONS[n]:
                 project(*PROJECTIONS[n])
-                round_projection(*PROJECTIONS[n])
-            if 0 <= n - FIRST_PIECE < len(PIECES):
-                begin_piece(*PIECES[n - FIRST_PIECE])
-            if 0 <= n - ROUND_LAG < len(PROJECTIONS) and (n - ROUND_LAG) % 2 == 1:
+            if n >= FIRST_PIECE:
+                for i, j in PIECES[len(begun) : min(len(begun) + PER_TURN, multiplied + AHEAD)]:
+                    if not {("aq", i), ("ak", 4 * j + 3)} <= quantized:
+                        break
+                    begin_piece(i, j)
+                    begun[i, j] = n
+            if 0 <= n - ROUND_LAG < len(PROJECTIONS) and PROJECTIONS[n - ROUND_LAG]:
                 side, i = PROJECTIONS[n - ROUND_LAG]
-                quantize_second(side, i // 2)
-            if 0 <= n - FIRST_PIECE - FINISH_LAG < len(PIECES):
-                multiply_piece(*PIECES[n - FIRST_PIECE - FINISH_LAG])
+                if side == "q" and i >= 4:
+                    quantize_second(side, i, 1)
+                elif i % 2 == 1:
+                    quantize_second(side, i - 1, 2)
+            ready = multiplied
+            for i, j in PIECES[ready : ready + PER_TURN]:
+                if begun.get((i, j), n) == n or not {("q", i), ("k", 4 * j + 3)} <= quantized:
+                    break
+                multiply_piece(i, j)
+                multiplied += 1
             for job in jobs.get(n, []):
-                job()
-            if 0 <= n - FIRST_PIECE - FINISH_LAG - 1 < len(PIECES):
-                store_piece(*PIECES[n - FIRST_PIECE - FINISH_LAG - 1])
+                job[0](*job[1:])
+            for piece in PIECES[stored:ready]:
+                store_piece(*piece)
+            stored = ready

@@ -209,8 +209,8 @@ def tile_featurepairqkscoreattribution_d2p_kernel(
         def project(side, i):
             codes, sc = first_q[i]
             bank = psum.tile([P, HALF], F32, name="bank")
-            for t in range(PACK):
-                for gg in range(2):
+            for gg in range(2):
+                for t in range(PACK):
                     at = P * (2 * slot[side] + gg)
                     nc.tensor.matmul_mx(
                         out=bank[:, P * t : P * t + P],
@@ -218,8 +218,8 @@ def tile_featurepairqkscoreattribution_d2p_kernel(
                         lhsT_scale=scales[side][:, 64 * t + 32 * gg : 64 * t + 32 * gg + 32].bitcast(U8),
                         rhs=codes[:, at : at + P].bitcast(FP8X4),
                         rhs_scale=sc[:, at : at + P],
-                        start=(gg == 0),
-                        stop=(gg == 1),
+                        start=(gg == 0 and t == 0),
+                        stop=(gg == 1 and t == PACK - 1),
                     )
             if i % 2 == 0:
                 second_in[side, i // 2] = work.tile([P, 2 * HALF], BF16, name="second_in", bufs=4, align_bytes=64)

@@ -108,20 +108,20 @@ def tile_featurepairqkscoreattribution_d2p_kernel(
         load_dq(1, 1)
         load_dk(0)
         load_dq(2, 2)
+        nc.sync.dma_start(out=head_rows[0:2, :], in_=head_w.bitcast(F32).rearrange("(w o) -> w o", o=1))
         load_dk(1)
         load_dk(2)
         load_dq(4, 2)
-        nc.sync.dma_start(out=head_rows[0:2, :], in_=head_w.bitcast(F32).rearrange("(w o) -> w o", o=1))
+        nc.sync.dma_start(out=g_in[:], in_=g.rearrange("(p t) -> p t", t=PACK))
         load_dk(3)
         load_words("k", wk_words)
         load_scales("k", wk_scales)
-        load_dq(6, 2)
         load_tokens(aq_in, aq, 0)
+        load_dq(6, 2)
         load_dk(4)
+        load_tokens(ak_in, ak, 0)
         load_words("q", wq_words)
         load_scales("q", wq_scales)
-        load_tokens(ak_in, ak, 0)
-        nc.sync.dma_start(out=g_in[:], in_=g.rearrange("(p t) -> p t", t=PACK))
         load_dk(5)
         load_dk(6)
         load_tokens(ak_in, ak, 1)
@@ -309,12 +309,12 @@ def tile_featurepairqkscoreattribution_d2p_kernel(
         turn_pair(0)
         widen(2)
         turn_pair(1)
+        spread_heads()
         widen(3)
         turn_pair(2)
         widen(4)
         quantize_first(0)
         turn_pair(3)
-        spread_heads()
         quantize_first(1)
         order_channels("k")
         widen(5)
@@ -323,17 +323,12 @@ def tile_featurepairqkscoreattribution_d2p_kernel(
 
         jobs = {
             0: [(widen, 6), (quantize_first, 3), (widen, 7), (interleave, "aq", 2, 1, on_scalar)],
-            1: [(turn_pair, 4), (order_channels, "q"), (multiply_g, 0), (interleave, "aq", 3, 1, on_vector)],
-            2: [
-                (interleave, "ak", 0, 2, on_vector),
-                (quantize_tokens, "aq", 0, 4),
-                (quantize_first, 4),
-                (interleave, "ak", 2, 2, on_vector),
-            ],
+            1: [(turn_pair, 4), (multiply_g, 0), (order_channels, "q"), (interleave, "aq", 3, 1, on_vector)],
+            2: [(interleave, "ak", 0, 4, on_vector), (quantize_tokens, "aq", 0, 4), (quantize_first, 4)],
             3: [(turn_pair, 5), (quantize_tokens, "ak", 0, 4)],
             4: [(multiply_g, 1), (quantize_first, 5)],
-            5: [(turn_pair, 6), (interleave, "ak", 4, 2, on_vector)],
-            6: [(interleave, "ak", 6, 2, on_vector), (quantize_first, 6)],
+            5: [(turn_pair, 6), (interleave, "ak", 4, 4, on_vector)],
+            6: [(quantize_first, 6)],
             7: [(turn_pair, 7)],
             8: [(quantize_tokens, "ak", 4, 4), (quantize_first, 7)],
             10: [(interleave, "aq", 4, 2, on_vector)],

@@ -26,6 +26,12 @@ P = 128
 PACK = 4
 HALF = 512
 TILES = N_FEAT // P
+COUPLES = (
+    [(("k", 0), ("q", 0)), (("q", 2), ("q", 1))]
+    + [(("k", i), ("q", i + 2)) for i in range(1, TILES - 2)]
+    + [(("k", TILES - 2), ("k", TILES - 1))]
+)
+EARLY = 4
 PROJECTIONS = (
     [(side, i) for side in ("k", "q") for i in range(4)]
     + [("k", i) for i in range(4, TILES)]
@@ -36,6 +42,9 @@ ROUND_LAG = 2
 FIRST_PIECE = 8
 PER_TURN = 2
 AHEAD = 3
+COUPLE_LEAD = 3
+FIRST_JOB = 2
+COUPLE_LAG = 2
 
 
 def tile_featurepairqkscoreattribution_d2p_kernel(
@@ -106,22 +115,21 @@ def tile_featurepairqkscoreattribution_d2p_kernel(
         nc.scalar.dma_start(out=scale_rows[0:64, :], in_=dq_scale.rearrange("i (j o) -> (i j) o", o=1))
         load_dq(0, 1)
         load_dq(1, 1)
-        load_dk(0)
-        load_dq(2, 2)
         nc.sync.dma_start(out=head_rows[0:2, :], in_=head_w.bitcast(F32).rearrange("(w o) -> w o", o=1))
-        load_dk(1)
+        for n in range(2):
+            load_dq(2 * n + 2, 2)
+            load_dk(n)
         load_dk(2)
-        load_dq(4, 2)
-        nc.sync.dma_start(out=g_in[:], in_=g.rearrange("(p t) -> p t", t=PACK))
-        load_dk(3)
         load_words("k", wk_words)
         load_scales("k", wk_scales)
-        load_tokens(aq_in, aq, 0)
         load_dq(6, 2)
+        load_dk(3)
         load_dk(4)
-        load_tokens(ak_in, ak, 0)
         load_words("q", wq_words)
         load_scales("q", wq_scales)
+        nc.sync.dma_start(out=g_in[:], in_=g.rearrange("(p t) -> p t", t=PACK))
+        load_tokens(ak_in, ak, 0)
+        load_tokens(aq_in, aq, 0)
         load_dk(5)
         load_dk(6)
         load_tokens(ak_in, ak, 1)
@@ -152,7 +160,6 @@ def tile_featurepairqkscoreattribution_d2p_kernel(
         dq_wide, first_in, first_q, second_in, bank_of = {}, {}, {}, {}, {}
         in_order_of_k = set()
         quantized = set()
-        slot = {"k": 0, "q": 1}
 
         def widen(i):
             dq_wide[i] = work.tile([P, WIDTH], BF16, name="wide", bufs=8)
@@ -177,41 +184,39 @@ def tile_featurepairqkscoreattribution_d2p_kernel(
                     scale=dq_sc[:, 8 * i + j : 8 * i + j + 1],
                 )
 
-        def turn(side, i):
-            pairs = (dk_in[i] if side == "k" else dq_wide[i])[:].bitcast(F32)
-            bank = psum.tile([P, HALF], F32, name="bank")
-            for gg in range(2):
-                for u in range(2):
-                    at = P * (2 * gg + u)
-                    if side == "k" or i in in_order_of_k:
-                        src = pairs[:, 2 * P * gg + u : 2 * P * gg + 2 * P : 2]
-                    else:
-                        src = pairs[:, at : at + P]
-                    nc.tensor.transpose(bank[:, at : at + P], src, ident[:])
-            if i not in first_in:
-                first_in[i] = work.tile([P, 2 * WIDTH], BF16, name="first_in", bufs=8, align_bytes=64)
-            dst = first_in[i][:, WIDTH * slot[side] : WIDTH * slot[side] + WIDTH]
-            nc.scalar.copy(
-                out=dst.bitcast(F32).rearrange("p (g f u) -> p g f u", g=2, u=2),
-                in_=bank[:].rearrange("p (g u f) -> p g f u", g=2, u=2),
-            )
+        def turn(n):
+            first_in[n] = work.tile([P, 2 * WIDTH], BF16, name="first_in", bufs=8, align_bytes=64)
+            for slot, (side, i) in enumerate(COUPLES[n]):
+                pairs = (dk_in[i] if side == "k" else dq_wide[i])[:].bitcast(F32)
+                bank = psum.tile([P, HALF], F32, name="bank")
+                for gg in range(2):
+                    for u in range(2):
+                        at = P * (2 * gg + u)
+                        if side == "k" or i in in_order_of_k:
+                            src = pairs[:, 2 * P * gg + u : 2 * P * gg + 2 * P : 2]
+                        else:
+                            src = pairs[:, at : at + P]
+                        nc.tensor.transpose(bank[:, at : at + P], src, ident[:])
+                dst = first_in[n][:, WIDTH * slot : WIDTH * slot + WIDTH]
+                nc.scalar.copy(
+                    out=dst.bitcast(F32).rearrange("p (g f u) -> p g f u", g=2, u=2),
+                    in_=bank[:].rearrange("p (g u f) -> p g f u", g=2, u=2),
+                )
 
-        def turn_pair(i):
-            turn("k", i)
-            turn("q", i)
-
-        def quantize_first(i):
+        def quantize_first(n):
             codes = work.tile([P, HALF], U32, name="codes1", bufs=8, align_bytes=64)
             sc = work.tile([P, HALF], U8, name="scales1", bufs=8, align_bytes=64)
-            nc.vector.quantize_mx(out=codes[:].bitcast(FP8X4), scales=sc[:], in_=first_in[i][:])
-            first_q[i] = (codes, sc)
+            nc.vector.quantize_mx(out=codes[:].bitcast(FP8X4), scales=sc[:], in_=first_in[n][:])
+            for slot, tile_of in enumerate(COUPLES[n]):
+                cols = slice(2 * P * slot, 2 * P * slot + 2 * P)
+                first_q[tile_of] = (codes[:, cols], sc[:, cols])
 
         def project(side, i):
-            codes, sc = first_q[i]
+            codes, sc = first_q[side, i]
             bank = psum.tile([P, HALF], F32, name="bank")
             for gg in range(2):
                 for t in range(PACK):
-                    at = P * (2 * slot[side] + gg)
+                    at = P * gg
                     nc.tensor.matmul_mx(
                         out=bank[:, P * t : P * t + P],
                         lhsT=words[side][:, 128 * t + 64 * gg : 128 * t + 64 * gg + 64].bitcast(FP4X4),
@@ -222,7 +227,7 @@ def tile_featurepairqkscoreattribution_d2p_kernel(
                         stop=(gg == 1 and t == PACK - 1),
                     )
             if i % 2 == 0:
-                second_in[side, i // 2] = work.tile([P, 2 * HALF], BF16, name="second_in", bufs=4, align_bytes=64)
+                second_in[side, i // 2] = work.tile([P, 2 * HALF], BF16, name="second_in", bufs=8, align_bytes=64)
             dst = second_in[side, i // 2][:, HALF * (i % 2) : HALF * (i % 2) + HALF].rearrange("p (f t) -> p f t", t=PACK)
             src = bank[:].rearrange("p (t f) -> p f t", t=PACK)
             if side == "k":
@@ -306,41 +311,42 @@ def tile_featurepairqkscoreattribution_d2p_kernel(
         spread_scales()
         widen(0)
         widen_on_scalar(1)
-        turn_pair(0)
-        widen(2)
-        turn_pair(1)
         spread_heads()
-        widen(3)
-        turn_pair(2)
-        widen(4)
-        quantize_first(0)
-        turn_pair(3)
-        quantize_first(1)
-        order_channels("k")
-        widen(5)
-        quantize_first(2)
-        interleave("aq", 0, 2, on_scalar)
+        for n in range(EARLY):
+            turn(n)
+            for side, i in COUPLES[n + 1]:
+                if side == "q" and i not in dq_wide:
+                    widen(i)
+            if n == 0:
+                widen(3)
+        between = [(order_channels, "k"), (widen, 6), (widen, 7), (order_channels, "q")]
+        for n in range(EARLY):
+            quantize_first(n)
+            between[n][0](*between[n][1:])
 
-        jobs = {
-            0: [(widen, 6), (quantize_first, 3), (widen, 7), (interleave, "aq", 2, 1, on_scalar)],
-            1: [(turn_pair, 4), (multiply_g, 0), (order_channels, "q"), (interleave, "aq", 3, 1, on_vector)],
-            2: [(interleave, "ak", 0, 4, on_vector), (quantize_tokens, "aq", 0, 4), (quantize_first, 4)],
-            3: [(turn_pair, 5), (quantize_tokens, "ak", 0, 4)],
-            4: [(multiply_g, 1), (quantize_first, 5)],
-            5: [(turn_pair, 6), (interleave, "ak", 4, 4, on_vector)],
-            6: [(quantize_first, 6)],
-            7: [(turn_pair, 7)],
-            8: [(quantize_tokens, "ak", 4, 4), (quantize_first, 7)],
-            10: [(interleave, "aq", 4, 2, on_vector)],
-            12: [(quantize_tokens, "aq", 4, 2)],
-            13: [(interleave, "aq", 6, 2, on_vector)],
-            15: [(quantize_tokens, "aq", 6, 2)],
-        }
+        jobs = [
+            [(multiply_g, 0)],
+            [(interleave, "ak", 0, 4, on_vector)],
+            [(interleave, "aq", 0, 1, on_scalar), (interleave, "aq", 1, 3, on_vector)],
+            [(quantize_tokens, "ak", 0, 4)],
+            [(multiply_g, 1)],
+            [(quantize_tokens, "aq", 0, 4)],
+            [(interleave, "ak", 4, 4, on_vector)],
+            [(interleave, "aq", 4, 2, on_vector)],
+            [(quantize_tokens, "ak", 4, 4)],
+            [(quantize_tokens, "aq", 4, 2), (interleave, "aq", 6, 2, on_vector)],
+            [(quantize_tokens, "aq", 6, 2)],
+        ]
 
+        turned_in = {n: EARLY + n for n in range(2)}
+        for c in range(EARLY + 2, len(COUPLES)):
+            turned_in[PROJECTIONS.index(COUPLES[c][0]) - COUPLE_LEAD] = c
         begun, multiplied, stored = {}, 0, 0
         for n in range(len(PROJECTIONS) + len(PIECES)):
             if n < len(PROJECTIONS) and PROJECTIONS[n]:
                 project(*PROJECTIONS[n])
+            if n in turned_in:
+                turn(turned_in[n])
             if n >= FIRST_PIECE:
                 for i, j in PIECES[len(begun) : min(len(begun) + PER_TURN, multiplied + AHEAD)]:
                     if not {("aq", i), ("ak", 4 * j + 3)} <= quantized:
@@ -359,8 +365,11 @@ def tile_featurepairqkscoreattribution_d2p_kernel(
                     break
                 multiply_piece(i, j)
                 multiplied += 1
-            for job in jobs.get(n, []):
-                job[0](*job[1:])
+            if n - COUPLE_LAG in turned_in:
+                quantize_first(turned_in[n - COUPLE_LAG])
+            if jobs and (FIRST_JOB <= n <= FIRST_PIECE or (n > FIRST_PIECE and n % 2 == 1)):
+                for job in jobs.pop(0):
+                    job[0](*job[1:])
             for piece in PIECES[stored:ready]:
                 store_piece(*piece)
             stored = ready

@@ -42,7 +42,7 @@ ROUND_LAG = 2
 FIRST_PIECE = 8
 PER_TURN = 2
 AHEAD = 3
-COUPLE_LEAD = 3
+COUPLE_LEAD = 4
 FIRST_JOB = 2
 COUPLE_LAG = 2
 
@@ -332,8 +332,8 @@ def tile_featurepairqkscoreattribution_d2p_kernel(
             [(multiply_g, 1)],
             [(quantize_tokens, "aq", 0, 4)],
             [(interleave, "ak", 4, 4, on_vector)],
-            [(interleave, "aq", 4, 2, on_vector)],
             [(quantize_tokens, "ak", 4, 4)],
+            [(interleave, "aq", 4, 2, on_vector)],
             [(quantize_tokens, "aq", 4, 2), (interleave, "aq", 6, 2, on_vector)],
             [(quantize_tokens, "aq", 6, 2)],
         ]
@@ -365,11 +365,11 @@ def tile_featurepairqkscoreattribution_d2p_kernel(
                     break
                 multiply_piece(i, j)
                 multiplied += 1
-            if n - COUPLE_LAG in turned_in:
-                quantize_first(turned_in[n - COUPLE_LAG])
             if jobs and (FIRST_JOB <= n <= FIRST_PIECE or (n > FIRST_PIECE and n % 2 == 1)):
                 for job in jobs.pop(0):
                     job[0](*job[1:])
+            if n - COUPLE_LAG in turned_in:
+                quantize_first(turned_in[n - COUPLE_LAG])
             for piece in PIECES[stored:ready]:
                 store_piece(*piece)
             stored = ready

@@ -53,42 +53,44 @@ def tile_featurepairqkscoreattribution_d2p_kernel(
     nc = tc.nc
     with ExitStack() as ctx:
         keep = ctx.enter_context(tc.tile_pool(name="keep", bufs=1))
-        work = ctx.enter_context(tc.tile_pool(name="work", bufs=4))
         psum = ctx.enter_context(tc.psum_pool(name="psum", bufs=8))
         ctx.enter_context(tc.manual_schedule())
 
-        ident = keep.tile([P, P], F32, name="ident")
-        dk_in = [keep.tile([P, WIDTH], BF16, name="dk_in%d" % i) for i in range(TILES)]
+        def tile(name, shape, dtype):
+            return keep.tile(shape, dtype, name=name, align_bytes=64)
+
+        ident = tile("ident", [P, P], F32)
+        dk_in = [tile("dk_in%d" % i, [P, WIDTH], BF16) for i in range(TILES)]
         dq_in = {}
-        scale_rows = keep.tile([P, 1], F32, name="scale_rows")
-        head_rows = keep.tile([P, 1], F32, name="head_rows")
-        dq_sc = keep.tile([P, 64], F32, name="dq_sc")
-        aq_in = [keep.tile([P, PACK, HALF], BF16, name="aq_in%d" % h) for h in range(2)]
-        ak_in = [keep.tile([P, PACK, HALF], BF16, name="ak_in%d" % h) for h in range(2)]
-        g_in = keep.tile([P, PACK], BF16, name="g_in")
-        head_col = keep.tile([P, 1], F32, name="head_col")
+        scale_rows = tile("scale_rows", [P, 1], F32)
+        head_rows = tile("head_rows", [P, 1], F32)
+        dq_sc = tile("dq_sc", [P, 64], F32)
+        aq_in = [tile("aq_in%d" % h, [P, PACK, HALF], BF16) for h in range(2)]
+        ak_in = [tile("ak_in%d" % h, [P, PACK, HALF], BF16) for h in range(2)]
+        g_in = tile("g_in", [P, PACK], BF16)
+        head_col = tile("head_col", [P, 1], F32)
         words_in, words, scales_in, scales = {}, {}, {}, {}
         for side in ("k", "q"):
-            words_in[side] = keep.tile([P, 512], I32, name="words_in_" + side, align_bytes=64)
-            words[side] = keep.tile([P, 512], I32, name="words_" + side, align_bytes=64)
-            scales_in[side] = keep.tile([P, 256], I32, name="scales_in_" + side, align_bytes=64)
-            scales[side] = keep.tile([P, 256], I32, name="scales_" + side, align_bytes=64)
+            words_in[side] = tile("words_in_" + side, [P, 512], I32)
+            words[side] = tile("words_" + side, [P, 512], I32)
+            scales_in[side] = tile("scales_in_" + side, [P, 256], I32)
+            scales[side] = tile("scales_" + side, [P, 256], I32)
         codes2, scales2 = {}, {}
         for name in ("k", "q", "aq", "ak"):
-            codes2[name] = keep.tile([P, N_FEAT], U32, name="codes2_" + name, align_bytes=64)
-            scales2[name] = keep.tile([P, N_FEAT], U8, name="scales2_" + name, align_bytes=64)
+            codes2[name] = tile("codes2_" + name, [P, N_FEAT], U32)
+            scales2[name] = tile("scales2_" + name, [P, N_FEAT], U8)
 
+        for side in ("k", "q"):
+            nc.vector.memset(scales_in[side][:], 0)
         nc.vector.memset(head_rows[:], 0.0)
         nc.vector.memset(scale_rows[64:P, :], 0.0)
-        for side in ("q", "k"):
-            nc.vector.memset(scales_in[side][:], 0)
         make_identity(nc, ident[:])
 
         def load_dk(i):
             nc.sync.dma_start(out=dk_in[i][:], in_=dk[P * i : P * i + P, :])
 
         def load_dq(first, count):
-            t = keep.tile([P, count, WIDTH], U8, name="dq_in%d" % first)
+            t = tile("dq_in%d" % first, [P, count, WIDTH], U8)
             rows = dq_bytes[P * first : P * (first + count), :]
             nc.sync.dma_start(out=t[:], in_=rows.rearrange("(a p) k -> p a k", p=P))
             for n in range(count):
@@ -157,12 +159,12 @@ def tile_featurepairqkscoreattribution_d2p_kernel(
                 rows = slice(32 * h, 32 * h + 32)
                 nc.scalar.activation(out=head_col[rows, 0:1], in_=head_in[rows, h : h + 1], func=COPY)
 
-        dq_wide, first_in, first_q, second_in, bank_of = {}, {}, {}, {}, {}
-        in_order_of_k = set()
+        dq_wide, first_in, first_q, second_in = {}, {}, {}, {}
         quantized = set()
+        in_order_of_k = set()
 
         def widen(i):
-            dq_wide[i] = work.tile([P, WIDTH], BF16, name="wide", bufs=8)
+            dq_wide[i] = tile("wide%d" % i, [P, WIDTH], BF16)
             by_pass = dq_wide[i][:].rearrange("p (g u m e) -> p g m u e", g=2, u=2, e=2)
             for j in range(8):
                 nc.vector.tensor_scalar(
@@ -174,7 +176,7 @@ def tile_featurepairqkscoreattribution_d2p_kernel(
                 )
 
         def widen_on_scalar(i):
-            dq_wide[i] = work.tile([P, WIDTH], BF16, name="wide", bufs=8)
+            dq_wide[i] = tile("wide%d" % i, [P, WIDTH], BF16)
             in_order_of_k.add(i)
             for j in range(8):
                 nc.scalar.activation(
@@ -184,9 +186,9 @@ def tile_featurepairqkscoreattribution_d2p_kernel(
                     scale=dq_sc[:, 8 * i + j : 8 * i + j + 1],
                 )
 
-        def turn(n):
-            first_in[n] = work.tile([P, 2 * WIDTH], BF16, name="first_in", bufs=8, align_bytes=64)
-            for slot, (side, i) in enumerate(COUPLES[n]):
+        def turn(*two):
+            first_in[two] = tile("first_in_%s%d" % two[0], [P, len(two) * WIDTH], BF16)
+            for n, (side, i) in enumerate(two):
                 pairs = (dk_in[i] if side == "k" else dq_wide[i])[:].bitcast(F32)
                 bank = psum.tile([P, HALF], F32, name="bank")
                 for gg in range(2):
@@ -197,38 +199,37 @@ def tile_featurepairqkscoreattribution_d2p_kernel(
                         else:
                             src = pairs[:, at : at + P]
                         nc.tensor.transpose(bank[:, at : at + P], src, ident[:])
-                dst = first_in[n][:, WIDTH * slot : WIDTH * slot + WIDTH]
+                dst = first_in[two][:, WIDTH * n : WIDTH * n + WIDTH]
                 nc.scalar.copy(
                     out=dst.bitcast(F32).rearrange("p (g f u) -> p g f u", g=2, u=2),
                     in_=bank[:].rearrange("p (g u f) -> p g f u", g=2, u=2),
                 )
 
-        def quantize_first(n):
-            codes = work.tile([P, HALF], U32, name="codes1", bufs=8, align_bytes=64)
-            sc = work.tile([P, HALF], U8, name="scales1", bufs=8, align_bytes=64)
-            nc.vector.quantize_mx(out=codes[:].bitcast(FP8X4), scales=sc[:], in_=first_in[n][:])
-            for slot, tile_of in enumerate(COUPLES[n]):
-                cols = slice(2 * P * slot, 2 * P * slot + 2 * P)
-                first_q[tile_of] = (codes[:, cols], sc[:, cols])
+        def quantize_first(*two):
+            codes = tile("codes1_%s%d" % two[0], [P, 2 * P * len(two)], U32)
+            sc = tile("scales1_%s%d" % two[0], [P, 2 * P * len(two)], U8)
+            nc.vector.quantize_mx(out=codes[:].bitcast(FP8X4), scales=sc[:], in_=first_in[two][:])
+            for n in range(len(two)):
+                first_q[two[n]] = (codes[:, 2 * P * n : 2 * P * (n + 1)], sc[:, 2 * P * n : 2 * P * (n + 1)])
 
         def project(side, i):
             codes, sc = first_q[side, i]
             bank = psum.tile([P, HALF], F32, name="bank")
             for gg in range(2):
                 for t in range(PACK):
-                    at = P * gg
                     nc.tensor.matmul_mx(
                         out=bank[:, P * t : P * t + P],
                         lhsT=words[side][:, 128 * t + 64 * gg : 128 * t + 64 * gg + 64].bitcast(FP4X4),
                         lhsT_scale=scales[side][:, 64 * t + 32 * gg : 64 * t + 32 * gg + 32].bitcast(U8),
-                        rhs=codes[:, at : at + P].bitcast(FP8X4),
-                        rhs_scale=sc[:, at : at + P],
+                        rhs=codes[:, P * gg : P * gg + P].bitcast(FP8X4),
+                        rhs_scale=sc[:, P * gg : P * gg + P],
                         start=(gg == 0 and t == 0),
                         stop=(gg == 1 and t == PACK - 1),
                     )
-            if i % 2 == 0:
-                second_in[side, i // 2] = work.tile([P, 2 * HALF], BF16, name="second_in", bufs=8, align_bytes=64)
-            dst = second_in[side, i // 2][:, HALF * (i % 2) : HALF * (i % 2) + HALF].rearrange("p (f t) -> p f t", t=PACK)
+            if (side, i // 2) not in second_in:
+                second_in[side, i // 2] = tile("second_in_%s%d" % (side, i // 2), [P, 2 * HALF], BF16)
+            at = HALF * (i % 2)
+            dst = second_in[side, i // 2][:, at : at + HALF].rearrange("p (f t) -> p f t", t=PACK)
             src = bank[:].rearrange("p (t f) -> p f t", t=PACK)
             if side == "k":
                 nc.scalar.copy(out=dst, in_=src)
@@ -236,7 +237,6 @@ def tile_featurepairqkscoreattribution_d2p_kernel(
                 nc.scalar.activation(out=dst, in_=src, func=COPY, scale=head_col[:, 0:1])
 
         def quantize_second(side, first, count):
-            quantized.update((side, i) for i in range(first, first + count))
             cols = slice(P * first, P * (first + count))
             at = HALF * (first % 2)
             nc.vector.quantize_mx(
@@ -244,11 +244,12 @@ def tile_featurepairqkscoreattribution_d2p_kernel(
                 scales=scales2[side][:, cols],
                 in_=second_in[side, first // 2][:, at : at + HALF * count],
             )
+            quantized.update((side, i) for i in range(first, first + count))
 
         ak_g, side_by_side = {}, {}
 
         def multiply_g(h):
-            ak_g[h] = work.tile([P, PACK, HALF], BF16, name="ak_g", bufs=2)
+            ak_g[h] = tile("ak_g%d" % h, [P, PACK, HALF], BF16)
             for t in range(PACK):
                 nc.vector.tensor_scalar(
                     out=ak_g[h][:, t, :], in0=ak_in[h][:, t, :], scalar1=g_in[:, t : t + 1], scalar2=None, op0=MULT
@@ -257,7 +258,7 @@ def tile_featurepairqkscoreattribution_d2p_kernel(
         def interleave(name, first, count, copy):
             h, at = first // 4, P * (first % 4)
             if (name, h) not in side_by_side:
-                side_by_side[name, h] = work.tile([P, PACK * HALF], BF16, name="side_by_side", bufs=4, align_bytes=64)
+                side_by_side[name, h] = tile("side_%s%d" % (name, h), [P, PACK * HALF], BF16)
             src = aq_in[h] if name == "aq" else ak_g[h]
             copy(
                 out=side_by_side[name, h][:, PACK * at : PACK * (at + P * count)].rearrange(
@@ -267,7 +268,6 @@ def tile_featurepairqkscoreattribution_d2p_kernel(
             )
 
         def quantize_tokens(name, first, count):
-            quantized.update((name, i) for i in range(first, first + count))
             cols = slice(P * first, P * (first + count))
             at = HALF * (first % 4)
             nc.vector.quantize_mx(
@@ -275,9 +275,10 @@ def tile_featurepairqkscoreattribution_d2p_kernel(
                 scales=scales2[name][:, cols],
                 in_=side_by_side[name, first // 4][:, at : at + HALF * count],
             )
+            quantized.update((name, i) for i in range(first, first + count))
 
         divisor = 1.0 / (TOKENS * math.sqrt(CHANNELS // HEADS))
-        c_part = {}
+        c_part, m_bank = {}, {}
 
         def product(rows, cols, i, j):
             bank = psum.tile([P, HALF], F32, name="bank")
@@ -294,16 +295,15 @@ def tile_featurepairqkscoreattribution_d2p_kernel(
 
         def begin_piece(i, j):
             bank = product("aq", "ak", i, j)
-            c_part[i, j] = work.tile([P, HALF], F32, name="c_part", bufs=12)
+            c_part[i, j] = keep.tile([P, HALF], F32, name="c_part", bufs=10)
             nc.scalar.activation(out=c_part[i, j][:], in_=bank[:], func=COPY, scale=divisor)
 
         def multiply_piece(i, j):
-            bank_of["m", i, j] = product("q", "k", i, j)
+            m_bank[i, j] = product("q", "k", i, j)
 
         def store_piece(i, j):
-            bank = bank_of["m", i, j]
-            piece = work.tile([P, HALF], F32, name="piece", bufs=8)
-            nc.vector.tensor_tensor(out=piece[:], in0=bank[:], in1=c_part[i, j][:], op=MULT)
+            piece = keep.tile([P, HALF], F32, name="piece", bufs=8)
+            nc.vector.tensor_tensor(out=piece[:], in0=m_bank[i, j][:], in1=c_part[i, j][:], op=MULT)
             nc.sync.dma_start(out=out[P * i : P * i + P, HALF * j : HALF * j + HALF], in_=piece[:])
 
         on_vector, on_scalar = nc.vector.tensor_copy, nc.scalar.copy
@@ -313,7 +313,7 @@ def tile_featurepairqkscoreattribution_d2p_kernel(
         widen_on_scalar(1)
         spread_heads()
         for n in range(EARLY):
-            turn(n)
+            turn(*COUPLES[n])
             for side, i in COUPLES[n + 1]:
                 if side == "q" and i not in dq_wide:
                     widen(i)
@@ -321,7 +321,7 @@ def tile_featurepairqkscoreattribution_d2p_kernel(
                 widen(3)
         between = [(order_channels, "k"), (widen, 6), (widen, 7), (order_channels, "q")]
         for n in range(EARLY):
-            quantize_first(n)
+            quantize_first(*COUPLES[n])
             between[n][0](*between[n][1:])
 
         jobs = [
@@ -346,7 +346,7 @@ def tile_featurepairqkscoreattribution_d2p_kernel(
             if n < len(PROJECTIONS) and PROJECTIONS[n]:
                 project(*PROJECTIONS[n])
             if n in turned_in:
-                turn(turned_in[n])
+                turn(*COUPLES[turned_in[n]])
             if n >= FIRST_PIECE:
                 for i, j in PIECES[len(begun) : min(len(begun) + PER_TURN, multiplied + AHEAD)]:
                     if not {("aq", i), ("ak", 4 * j + 3)} <= quantized:
@@ -369,7 +369,7 @@ def tile_featurepairqkscoreattribution_d2p_kernel(
                 for job in jobs.pop(0):
                     job[0](*job[1:])
             if n - COUPLE_LAG in turned_in:
-                quantize_first(turned_in[n - COUPLE_LAG])
+                quantize_first(*COUPLES[turned_in[n - COUPLE_LAG]])
             for piece in PIECES[stored:ready]:
                 store_piece(*piece)
             stored = ready

@@ -85,6 +85,8 @@ def tile_featurepairqkscoreattribution_d2p_kernel(
         nc.vector.memset(head_rows[:], 0.0)
         nc.vector.memset(scale_rows[64:P, :], 0.0)
         make_identity(nc, ident[:])
+        idle = tile("idle", [P, HALF], BF16)
+        nc.vector.memset(idle[:], 0.0)
 
         def load_dk(i):
             nc.sync.dma_start(out=dk_in[i][:], in_=dk[P * i : P * i + P, :])
@@ -306,14 +308,22 @@ def tile_featurepairqkscoreattribution_d2p_kernel(
             nc.vector.tensor_tensor(out=piece[:], in0=m_bank[i, j][:], in1=c_part[i, j][:], op=MULT)
             nc.sync.dma_start(out=out[P * i : P * i + P, HALF * j : HALF * j + HALF], in_=piece[:])
 
+        def warm_up(count):
+            bank = psum.tile([P, HALF], F32, name="bank")
+            for n in range(count):
+                nc.tensor.matmul(bank[:], lhsT=idle[:, 0:P], rhs=idle[:], start=(n == 0), stop=(n == count - 1))
+
         on_vector, on_scalar = nc.vector.tensor_copy, nc.scalar.copy
 
         spread_scales()
         widen(0)
         widen_on_scalar(1)
         spread_heads()
+        warm_up(3)
         for n in range(EARLY):
             turn(*COUPLES[n])
+            if n == EARLY - 1:
+                warm_up(2)
             for side, i in COUPLES[n + 1]:
                 if side == "q" and i not in dq_wide:
                     widen(i)

@@ -43,7 +43,7 @@ FIRST_PIECE = 8
 PER_TURN = 2
 AHEAD = 3
 COUPLE_LEAD = 4
-FIRST_JOB = 2
+FIRST_JOB = 3
 COUPLE_LAG = 2
 
 
@@ -60,7 +60,7 @@ def tile_featurepairqkscoreattribution_d2p_kernel(
             return keep.tile(shape, dtype, name=name, align_bytes=64)
 
         ident = tile("ident", [P, P], F32)
-        dk_in = [tile("dk_in%d" % i, [P, WIDTH], BF16) for i in range(TILES)]
+        dk_in = {}
         dq_in = {}
         scale_rows = tile("scale_rows", [P, 1], F32)
         head_rows = tile("head_rows", [P, 1], F32)
@@ -88,8 +88,12 @@ def tile_featurepairqkscoreattribution_d2p_kernel(
         idle = tile("idle", [P, HALF], BF16)
         nc.vector.memset(idle[:], 0.0)
 
-        def load_dk(i):
-            nc.sync.dma_start(out=dk_in[i][:], in_=dk[P * i : P * i + P, :])
+        def load_dk(first, count=1):
+            t = tile("dk_in%d" % first, [P, count * WIDTH], BF16)
+            rows = dk[P * first : P * (first + count), :]
+            nc.sync.dma_start(out=t[:].rearrange("p (a k) -> p a k", a=count), in_=rows.rearrange("(a p) k -> p a k", p=P))
+            for n in range(count):
+                dk_in[first + n] = t[:, WIDTH * n : WIDTH * (n + 1)]
 
         def load_dq(first, count):
             t = tile("dq_in%d" % first, [P, count, WIDTH], U8)
@@ -124,15 +128,14 @@ def tile_featurepairqkscoreattribution_d2p_kernel(
             load_dq(2 * n + 2, 2)
             load_dk(n)
         load_dk(2)
+        nc.sync.dma_start(out=g_in[:], in_=g.rearrange("(p t) -> p t", t=PACK))
         load_words("k", wk_words)
         load_scales("k", wk_scales)
         load_dq(6, 2)
-        load_dk(3)
-        load_dk(4)
+        load_dk(3, 2)
         load_words("q", wq_words)
-        load_scales("q", wq_scales)
-        nc.sync.dma_start(out=g_in[:], in_=g.rearrange("(p t) -> p t", t=PACK))
         load_tokens(ak_in, ak, 0)
+        load_scales("q", wq_scales)
         load_tokens(aq_in, aq, 0)
         load_dk(5)
         load_dk(6)
@@ -329,14 +332,13 @@ def tile_featurepairqkscoreattribution_d2p_kernel(
                     widen(i)
             if n == 0:
                 widen(3)
-        between = [(order_channels, "k"), (widen, 6), (widen, 7), (order_channels, "q")]
+        between = [(order_channels, "k"), (widen, 6), (widen, 7), (multiply_g, 0)]
         for n in range(EARLY):
             quantize_first(*COUPLES[n])
             between[n][0](*between[n][1:])
 
         jobs = [
-            [(multiply_g, 0)],
-            [(interleave, "ak", 0, 4, on_vector)],
+            [(order_channels, "q"), (interleave, "ak", 0, 4, on_vector)],
             [(interleave, "aq", 0, 1, on_scalar), (interleave, "aq", 1, 3, on_vector)],
             [(quantize_tokens, "ak", 0, 4)],
             [(multiply_g, 1)],

@@ -321,8 +321,8 @@ def tile_featurepairqkscoreattribution_d2p_kernel(
         spread_scales()
         widen(0)
         widen_on_scalar(1)
-        spread_heads()
         warm_up(3)
+        spread_heads()
         for n in range(EARLY):
             turn(*COUPLES[n])
             if n == EARLY - 1:

@@ -128,13 +128,13 @@ def tile_featurepairqkscoreattribution_d2p_kernel(
             load_dq(2 * n + 2, 2)
             load_dk(n)
         load_dk(2)
-        nc.sync.dma_start(out=g_in[:], in_=g.rearrange("(p t) -> p t", t=PACK))
         load_words("k", wk_words)
         load_scales("k", wk_scales)
         load_dq(6, 2)
         load_dk(3, 2)
-        load_words("q", wq_words)
+        nc.sync.dma_start(out=g_in[:], in_=g.rearrange("(p t) -> p t", t=PACK))
         load_tokens(ak_in, ak, 0)
+        load_words("q", wq_words)
         load_scales("q", wq_scales)
         load_tokens(aq_in, aq, 0)
         load_dk(5)

import math
from contextlib import ExitStack

import concourse.mybir as mybir
from concourse.masks import make_identity

N_FEAT = 1024
WIDTH = 1024
CHANNELS = 512
HEADS = 4
TOKENS = 512
FLOPS = 2 * N_FEAT * (2 * WIDTH * CHANNELS + N_FEAT * CHANNELS + N_FEAT * TOKENS)

F32 = mybir.dt.float32
BF16 = mybir.dt.bfloat16
I32 = mybir.dt.int32
U32 = mybir.dt.uint32
U8 = mybir.dt.uint8
FP8 = mybir.dt.float8_e4m3fn
FP8X4 = mybir.dt.float8_e4m3fn_x4
FP4X4 = mybir.dt.float4_e2m1fn_x4
MULT = mybir.AluOpType.mult
COPY = mybir.ActivationFunctionType.Copy

P = 128
PACK = 4
HALF = 512
TILES = N_FEAT // P
COUPLES = (
    [(("k", 0), ("q", 0)), (("q", 2), ("q", 1))]
    + [(("k", i), ("q", i + 2)) for i in range(1, TILES - 2)]
    + [(("k", TILES - 2), ("k", TILES - 1))]
)
EARLY = 4
PROJECTIONS = (
    [(side, i) for side in ("k", "q") for i in range(4)]
    + [("k", i) for i in range(4, TILES)]
    + [("q", 4), ("q", 5), None, ("q", 6), None, ("q", 7)]
)
PIECES = [(i, j) for j in range(2) for i in range(4)] + [(i, j) for i in range(4, TILES) for j in range(2)]
ROUND_LAG = 2
FIRST_PIECE = 8
PER_TURN = 2
AHEAD = 3
COUPLE_LEAD = 4
FIRST_JOB = 3
COUPLE_LAG = 2


def tile_featurepairqkscoreattribution_d2p_kernel(
    tc, dq_bytes, dq_scale, dk, wq_words, wq_scales, wk_words, wk_scales, head_w, aq, ak, g, out
):
    nc = tc.nc
    with ExitStack() as ctx:
        keep = ctx.enter_context(tc.tile_pool(name="keep", bufs=1))
        psum = ctx.enter_context(tc.psum_pool(name="psum", bufs=8))
        ctx.enter_context(tc.manual_schedule())

        def tile(name, shape, dtype):
            return keep.tile(shape, dtype, name=name, align_bytes=64)

        ident = tile("ident", [P, P], F32)
        dk_in = {}
        dq_in = {}
        scale_rows = tile("scale_rows", [P, 1], F32)
        head_rows = tile("head_rows", [P, 1], F32)
        dq_sc = tile("dq_sc", [P, 64], F32)
        aq_in = [tile("aq_in%d" % h, [P, PACK, HALF], BF16) for h in range(2)]
        ak_in = [tile("ak_in%d" % h, [P, PACK, HALF], BF16) for h in range(2)]
        g_in = tile("g_in", [P, PACK], BF16)
        head_col = tile("head_col", [P, 1], F32)
        words_in, words, scales_in, scales = {}, {}, {}, {}
        for side in ("k", "q"):
            words_in[side] = tile("words_in_" + side, [P, 512], I32)
            words[side] = tile("words_" + side, [P, 512], I32)
            scales_in[side] = tile("scales_in_" + side, [P, 256], I32)
            scales[side] = tile("scales_" + side, [P, 256], I32)
        codes2, scales2 = {}, {}
        for name in ("k", "q", "aq", "ak"):
            codes2[name] = tile("codes2_" + name, [P, N_FEAT], U32)
            scales2[name] = tile("scales2_" + name, [P, N_FEAT], U8)

        for side in ("k", "q"):
            nc.vector.memset(scales_in[side][:], 0)
        nc.vector.memset(head_rows[:], 0.0)
        nc.vector.memset(scale_rows[64:P, :], 0.0)
        make_identity(nc, ident[:])
        idle = tile("idle", [P, HALF], BF16)
        nc.vector.memset(idle[:], 0.0)

        def load_dk(first, count=1):
            t = tile("dk_in%d" % first, [P, count * WIDTH], BF16)
            rows = dk[P * first : P * (first + count), :]
            nc.sync.dma_start(out=t[:].rearrange("p (a k) -> p a k", a=count), in_=rows.rearrange("(a p) k -> p a k", p=P))
            for n in range(count):
                dk_in[first + n] = t[:, WIDTH * n : WIDTH * (n + 1)]

        def load_dq(first, count):
            t = tile("dq_in%d" % first, [P, count, WIDTH], U8)
            rows = dq_bytes[P * first : P * (first + count), :]
            nc.sync.dma_start(out=t[:], in_=rows.rearrange("(a p) k -> p a k", p=P))
            for n in range(count):
                dq_in[first + n] = t[:, n, :]

        def load_tokens(dst, src, h):
            cols = src[:, HALF * h : HALF * h + HALF]
            nc.sync.dma_start(out=dst[h][:], in_=cols.rearrange("(p t) w -> p t w", t=PACK))

        def load_words(side, src):
            nc.sync.dma_start(
                out=words_in[side][:].rearrange("p (g n) -> p g n", g=2),
                in_=src.bitcast(I32).rearrange("g p n -> p g n"),
            )

        def load_scales(side, src):
            rows = src.bitcast(I32)
            for r in range(4):
                nc.sync.dma_start(
                    out=scales_in[side][r:P:32, :].rearrange("q (g n) -> q g n", g=2),
                    in_=rows[:, r:16:4, :].rearrange("g q n -> q g n"),
                )

        nc.scalar.dma_start(out=scale_rows[0:64, :], in_=dq_scale.rearrange("i (j o) -> (i j) o", o=1))
        load_dq(0, 1)
        load_dq(1, 1)
        nc.sync.dma_start(out=head_rows[0:2, :], in_=head_w.bitcast(F32).rearrange("(w o) -> w o", o=1))
        for n in range(2):
            load_dq(2 * n + 2, 2)
            load_dk(n)
        load_dk(2)
        load_words("k", wk_words)
        load_scales("k", wk_scales)
        load_dq(6, 2)
        load_dk(3, 2)
        nc.sync.dma_start(out=g_in[:], in_=g.rearrange("(p t) -> p t", t=PACK))
        load_tokens(ak_in, ak, 0)
        load_words("q", wq_words)
        load_scales("q", wq_scales)
        load_tokens(aq_in, aq, 0)
        load_dk(5)
        load_dk(6)
        load_tokens(ak_in, ak, 1)
        load_dk(7)
        load_tokens(aq_in, aq, 1)

        def order_channels(side):
            for dst, src, run in ((words, words_in, 4), (scales, scales_in, 2)):
                nc.vector.tensor_copy(
                    out=dst[side][:].rearrange("p (t x w) -> p t x w", t=4, w=run),
                    in_=src[side][:].rearrange("p (x t w) -> p t x w", t=4, w=run),
                )

        def along_partitions(rows):
            bank = psum.tile([P, HALF], F32, name="bank")
            nc.tensor.transpose(bank[:, 0:P], rows[:, 0:1].to_broadcast([P, P]), ident[:])
            return bank

        def spread_scales():
            nc.scalar.activation(out=dq_sc[:], in_=along_partitions(scale_rows)[:, 0:64], func=COPY)

        def spread_heads():
            head_in = along_partitions(head_rows)[:, 0:2].bitcast(BF16)
            for h in range(HEADS):
                rows = slice(32 * h, 32 * h + 32)
                nc.scalar.activation(out=head_col[rows, 0:1], in_=head_in[rows, h : h + 1], func=COPY)

        dq_wide, first_in, first_q, second_in = {}, {}, {}, {}
        quantized = set()
        in_order_of_k = set()

        def widen(i):
            dq_wide[i] = tile("wide%d" % i, [P, WIDTH], BF16)
            by_pass = dq_wide[i][:].rearrange("p (g u m e) -> p g m u e", g=2, u=2, e=2)
            for j in range(8):
                nc.vector.tensor_scalar(
                    out=by_pass[:, j // 4, 32 * (j % 4) : 32 * (j % 4) + 32, :, :],
                    in0=dq_in[i][:, P * j : P * j + P].bitcast(FP8),
                    scalar1=dq_sc[:, 8 * i + j : 8 * i + j + 1],
                    scalar2=None,
                    op0=MULT,
                )

        def widen_on_scalar(i):
            dq_wide[i] = tile("wide%d" % i, [P, WIDTH], BF16)
            in_order_of_k.add(i)
            for j in range(8):
                nc.scalar.activation(
                    out=dq_wide[i][:, P * j : P * j + P],
                    in_=dq_in[i][:, P * j : P * j + P].bitcast(FP8),
                    func=COPY,
                    scale=dq_sc[:, 8 * i + j : 8 * i + j + 1],
                )

        def turn(*two):
            first_in[two] = tile("first_in_%s%d" % two[0], [P, len(two) * WIDTH], BF16)
            for n, (side, i) in enumerate(two):
                pairs = (dk_in[i] if side == "k" else dq_wide[i])[:].bitcast(F32)
                bank = psum.tile([P, HALF], F32, name="bank")
                for gg in range(2):
                    for u in range(2):
                        at = P * (2 * gg + u)
                        if side == "k" or i in in_order_of_k:
                            src = pairs[:, 2 * P * gg + u : 2 * P * gg + 2 * P : 2]
                        else:
                            src = pairs[:, at : at + P]
                        nc.tensor.transpose(bank[:, at : at + P], src, ident[:])
                dst = first_in[two][:, WIDTH * n : WIDTH * n + WIDTH]
                nc.scalar.copy(
                    out=dst.bitcast(F32).rearrange("p (g f u) -> p g f u", g=2, u=2),
                    in_=bank[:].rearrange("p (g u f) -> p g f u", g=2, u=2),
                )

        def quantize_first(*two):
            codes = tile("codes1_%s%d" % two[0], [P, 2 * P * len(two)], U32)
            sc = tile("scales1_%s%d" % two[0], [P, 2 * P * len(two)], U8)
            nc.vector.quantize_mx(out=codes[:].bitcast(FP8X4), scales=sc[:], in_=first_in[two][:])
            for n in range(len(two)):
                first_q[two[n]] = (codes[:, 2 * P * n : 2 * P * (n + 1)], sc[:, 2 * P * n : 2 * P * (n + 1)])

        def project(side, i):
            codes, sc = first_q[side, i]
            bank = psum.tile([P, HALF], F32, name="bank")
            for gg in range(2):
                for t in range(PACK):
                    nc.tensor.matmul_mx(
                        out=bank[:, P * t : P * t + P],
                        lhsT=words[side][:, 128 * t + 64 * gg : 128 * t + 64 * gg + 64].bitcast(FP4X4),
                        lhsT_scale=scales[side][:, 64 * t + 32 * gg : 64 * t + 32 * gg + 32].bitcast(U8),
                        rhs=codes[:, P * gg : P * gg + P].bitcast(FP8X4),
                        rhs_scale=sc[:, P * gg : P * gg + P],
                        start=(gg == 0 and t == 0),
                        stop=(gg == 1 and t == PACK - 1),
                    )
            if (side, i // 2) not in second_in:
                second_in[side, i // 2] = tile("second_in_%s%d" % (side, i // 2), [P, 2 * HALF], BF16)
            at = HALF * (i % 2)
            dst = second_in[side, i // 2][:, at : at + HALF].rearrange("p (f t) -> p f t", t=PACK)
            src = bank[:].rearrange("p (t f) -> p f t", t=PACK)
            if side == "k":
                nc.scalar.copy(out=dst, in_=src)
            else:
                nc.scalar.activation(out=dst, in_=src, func=COPY, scale=head_col[:, 0:1])

        def quantize_second(side, first, count):
            cols = slice(P * first, P * (first + count))
            at = HALF * (first % 2)
            nc.vector.quantize_mx(
                out=codes2[side][:, cols].bitcast(FP8X4),
                scales=scales2[side][:, cols],
                in_=second_in[side, first // 2][:, at : at + HALF * count],
            )
            quantized.update((side, i) for i in range(first, first + count))

        ak_g, side_by_side = {}, {}

        def multiply_g(h):
            ak_g[h] = tile("ak_g%d" % h, [P, PACK, HALF], BF16)
            for t in range(PACK):
                nc.vector.tensor_scalar(
                    out=ak_g[h][:, t, :], in0=ak_in[h][:, t, :], scalar1=g_in[:, t : t + 1], scalar2=None, op0=MULT
                )

        def interleave(name, first, count, copy):
            h, at = first // 4, P * (first % 4)
            if (name, h) not in side_by_side:
                side_by_side[name, h] = tile("side_%s%d" % (name, h), [P, PACK * HALF], BF16)
            src = aq_in[h] if name == "aq" else ak_g[h]
            copy(
                out=side_by_side[name, h][:, PACK * at : PACK * (at + P * count)].rearrange(
                    "p (c i t) -> p c t i", i=4, t=PACK
                ),
                in_=src[:, :, at : at + P * count].rearrange("p t (c i) -> p c t i", i=4),
            )

        def quantize_tokens(name, first, count):
            cols = slice(P * first, P * (first + count))
            at = HALF * (first % 4)
            nc.vector.quantize_mx(
                out=codes2[name][:, cols].bitcast(FP8X4),
                scales=scales2[name][:, cols],
                in_=side_by_side[name, first // 4][:, at : at + HALF * count],
            )
            quantized.update((name, i) for i in range(first, first + count))

        divisor = 1.0 / (TOKENS * math.sqrt(CHANNELS // HEADS))
        c_part, m_bank = {}, {}

        def product(rows, cols, i, j):
            bank = psum.tile([P, HALF], F32, name="bank")
            nc.tensor.matmul_mx(
                out=bank[:],
                lhsT=codes2[rows][:, P * i : P * i + P].bitcast(FP8X4),
                lhsT_scale=scales2[rows][:, P * i : P * i + P],
                rhs=codes2[cols][:, HALF * j : HALF * j + HALF].bitcast(FP8X4),
                rhs_scale=scales2[cols][:, HALF * j : HALF * j + HALF],
                start=True,
                stop=True,
            )
            return bank

        def begin_piece(i, j):
            bank = product("aq", "ak", i, j)
            c_part[i, j] = keep.tile([P, HALF], F32, name="c_part", bufs=10)
            nc.scalar.activation(out=c_part[i, j][:], in_=bank[:], func=COPY, scale=divisor)

        def multiply_piece(i, j):
            m_bank[i, j] = product("q", "k", i, j)

        def store_piece(i, j):
            piece = keep.tile([P, HALF], F32, name="piece", bufs=8)
            nc.vector.tensor_tensor(out=piece[:], in0=m_bank[i, j][:], in1=c_part[i, j][:], op=MULT)
            nc.sync.dma_start(out=out[P * i : P * i + P, HALF * j : HALF * j + HALF], in_=piece[:])

        def warm_up(count):
            bank = psum.tile([P, HALF], F32, name="bank")
            for n in range(count):
                nc.tensor.matmul(bank[:], lhsT=idle[:, 0:P], rhs=idle[:], start=(n == 0), stop=(n == count - 1))

        on_vector, on_scalar = nc.vector.tensor_copy, nc.scalar.copy

        spread_scales()
        widen(0)
        widen_on_scalar(1)
        warm_up(3)
        spread_heads()
        for n in range(EARLY):
            turn(*COUPLES[n])
            if n == EARLY - 1:
                warm_up(2)
            for side, i in COUPLES[n + 1]:
                if side == "q" and i not in dq_wide:
                    widen(i)
            if n == 0:
                widen(3)
        between = [(order_channels, "k"), (widen, 6), (widen, 7), (multiply_g, 0)]
        for n in range(EARLY):
            quantize_first(*COUPLES[n])
            between[n][0](*between[n][1:])

        jobs = [
            [(order_channels, "q"), (interleave, "ak", 0, 4, on_vector)],
            [(interleave, "aq", 0, 1, on_scalar), (interleave, "aq", 1, 3, on_vector)],
            [(quantize_tokens, "ak", 0, 4)],
            [(multiply_g, 1)],
            [(quantize_tokens, "aq", 0, 4)],
            [(interleave, "ak", 4, 4, on_vector)],
            [(quantize_tokens, "ak", 4, 4)],
            [(interleave, "aq", 4, 2, on_vector)],
            [(quantize_tokens, "aq", 4, 2), (interleave, "aq", 6, 2, on_vector)],
            [(quantize_tokens, "aq", 6, 2)],
        ]

        turned_in = {n: EARLY + n for n in range(2)}
        for c in range(EARLY + 2, len(COUPLES)):
            turned_in[PROJECTIONS.index(COUPLES[c][0]) - COUPLE_LEAD] = c
        begun, multiplied, stored = {}, 0, 0
        for n in range(len(PROJECTIONS) + len(PIECES)):
            if n < len(PROJECTIONS) and PROJECTIONS[n]:
                project(*PROJECTIONS[n])
            if n in turned_in:
                turn(*COUPLES[turned_in[n]])
            if n >= FIRST_PIECE:
                for i, j in PIECES[len(begun) : min(len(begun) + PER_TURN, multiplied + AHEAD)]:
                    if not {("aq", i), ("ak", 4 * j + 3)} <= quantized:
                        break
                    begin_piece(i, j)
                    begun[i, j] = n
            if 0 <= n - ROUND_LAG < len(PROJECTIONS) and PROJECTIONS[n - ROUND_LAG]:
                side, i = PROJECTIONS[n - ROUND_LAG]
                if side == "q" and i >= 4:
                    quantize_second(side, i, 1)
                elif i % 2 == 1:
                    quantize_second(side, i - 1, 2)
            ready = multiplied
            for i, j in PIECES[ready : ready + PER_TURN]:
                if begun.get((i, j), n) == n or not {("q", i), ("k", 4 * j + 3)} <= quantized:
                    break
                multiply_piece(i, j)
                multiplied += 1
            if jobs and (FIRST_JOB <= n <= FIRST_PIECE or (n > FIRST_PIECE and n % 2 == 1)):
                for job in jobs.pop(0):
                    job[0](*job[1:])
            if n - COUPLE_LAG in turned_in:
                quantize_first(*COUPLES[turned_in[n - COUPLE_LAG]])
            for piece in PIECES[stored:ready]:
                store_piece(*piece)
            stored = ready
